import numpy as np
import ml_dtypes


def mxq(x, axis, fmt="e4m3"):
    dtype, down = {"e4m3": (ml_dtypes.float8_e4m3fn, 7), "e5m2": (ml_dtypes.float8_e5m2, 14)}[fmt]
    v = np.moveaxis(np.asarray(x, np.float32).astype(ml_dtypes.bfloat16).astype(np.float64), axis, -1)
    blocks = v.reshape(v.shape[:-1] + (-1, 32))
    amax = np.abs(blocks).max(-1, keepdims=True)
    byte = np.maximum(np.where(amax > 0, np.frexp(amax)[1] - 1 + 127, 0) - down, 1)
    scale = np.exp2(byte - 127.0)
    codes = (blocks / scale).astype(np.float32).astype(dtype).astype(np.float64)
    return np.moveaxis((codes * scale).reshape(v.shape), -1, axis)


WIDE = False


def mx_kscale(k):
    if not WIDE:
        return np.ones(k)
    levels = np.array([10, -10, 5, -5, 0])
    if k % 512:
        return np.exp2(np.random.permutation(np.resize(levels, k // 32))).repeat(32)
    a = np.empty((k // 512, 16))
    for p in range(k // 512):
        a[p, :8] = np.random.permutation(np.resize(levels, 8))
        for g in range(8):
            far = levels[np.abs(levels - a[p, g]) >= 10]
            a[p, g + 8] = far[np.random.randint(len(far))]
    return np.exp2(a.ravel()).repeat(32)


def f64(x):
    return np.asarray(x).astype(np.float64)


def striped(idx):
    return np.tile(idx.reshape(-1, 16).T, (8, 1)).astype(np.uint16)


def unstriped(offs):
    return offs[:16].T.reshape(-1).astype(np.int64)


E2M1 = np.array([0.0, 0.5, 1.0, 1.5, 2.0, 3.0, 4.0, 6.0, -0.0, -0.5, -1.0, -1.5, -2.0, -3.0, -4.0, -6.0])


def pack_weight(w, fmt):
    k, n = w.shape
    w = f64(np.asarray(w, np.float32).astype(ml_dtypes.bfloat16)).reshape(k // 32, 32, n)
    amax = np.abs(w).max(1)
    if fmt == "e4m3":
        byte = np.frexp(amax)[1] - 1 + 127 - 7
    else:
        mant, ex = np.frexp(amax / 6.0)
        byte = np.where(mant > 0.5, ex, ex - 1) + 127
    byte = np.clip(np.where(amax > 0, byte, 1), 1, 254)
    scaled = (w * np.exp2(127.0 - byte)[:, None, :]).reshape(k, n).astype(np.float32)
    by_word = np.ascontiguousarray(scaled.reshape(k // 512, 128, 4, n).transpose(0, 1, 3, 2))
    if fmt == "e4m3":
        words = by_word.astype(ml_dtypes.float8_e4m3fn).view(np.uint8)
    else:
        c = by_word.astype(ml_dtypes.float4_e2m1fn).view(np.uint8) & 0xF
        words = (c[..., 0::2] | (c[..., 1::2] << 4)).reshape(k // 512, 128, 2 * n)
    return np.ascontiguousarray(words), np.ascontiguousarray(byte.astype(np.uint8).reshape(k // 512, 16, n))


def unpack_weight(words, scales, fmt):
    g, _, n = scales.shape
    words = np.ascontiguousarray(words).reshape(g, 128, n, -1)
    if fmt == "e4m3":
        vals = words.view(ml_dtypes.float8_e4m3fn).astype(np.float64)
    else:
        nib = np.empty((g, 128, n, 4), np.uint8)
        nib[..., 0::2] = words & 0xF
        nib[..., 1::2] = words >> 4
        vals = E2M1[nib]
    vals = vals * np.repeat(np.exp2(scales.astype(np.float64) - 127.0), 8, axis=1)[..., None]
    return vals.transpose(0, 1, 3, 2).reshape(g * 512, n)


def gelu(v):
    return 0.5 * v * (1.0 + np.tanh(np.sqrt(2.0 / np.pi) * (v + 0.044715 * v**3)))


K, H, T, S, P = 512, 1024, 4096, 1024, 512

def setup_inputs():
    n = np.random.standard_normal
    s = mx_kscale(K)[:, None]
    u = mx_kscale(H)[:, None]
    tab_words, tab_scales = pack_weight(n((K, T)) * s, "e4m3")
    w2_words, w2_scales = pack_weight(0.8 * n((K, H)) / s / np.sqrt(K), "e2m1")
    return {
        "tab_words": tab_words, "tab_scales": tab_scales,
        "offs": striped(np.random.permutation(T)[:S]),
        "pos1": striped(np.random.permutation(S)[:P]),
        "pos2": striped(np.random.permutation(S)[:P]),
        "w1": (2.0 * n((K, H)) / s / np.sqrt(K)).astype(np.float32),
        "w2_words": w2_words, "w2_scales": w2_scales,
        "w3": (1.4 * n((K, H)) / s / u.T / np.sqrt(K * H)).astype(np.float32),
        "gain": (np.exp(0.3 * n(H)) * u[:, 0]).astype(np.float32),
        "shift": (0.8 * n(H) * u[:, 0]).astype(np.float32),
        "wt": (n(H) / u[:, 0] ** 2 / np.sqrt(H)).astype(np.float32),
        "rel": np.exp(0.3 * n(P)).astype(np.float32),
    }

def reference(tab_words, tab_scales, offs, pos1, pos2, w1, w2_words, w2_scales, w3, gain, shift, wt, rel):
    v = unpack_weight(tab_words, tab_scales, "e4m3")[:, unstriped(offs)]
    w2 = unpack_weight(w2_words, w2_scales, "e2m1")
    bent = np.tanh(mxq(f64(w1), 0, "e4m3").T @ v)
    straight = w2.T @ v
    h = (bent + straight) * f64(gain)[:, None]
    view = mxq(f64(w3), 0, "e4m3").T @ v
    x1 = mxq(h[:, unstriped(pos1)], 0, "e4m3")
    x2 = mxq((h[:, unstriped(pos2)] + f64(shift)[:, None]) * f64(wt)[:, None], 0, "e4m3")
    x3 = mxq(view[:, unstriped(pos2)], 0, "e4m3")
    e = x1.T @ x2
    e3 = x1.T @ x3
    return np.maximum(e, e3) * f64(rel)[None, :]

@@ -1,0 +1,251 @@
+from contextlib import ExitStack
+
+import concourse.mybir as mybir
+
+K, H, T, S, L = 512, 1024, 4096, 1024, 512
+FLOPS = 3 * 2 * K * H * S + 2 * 2 * H * L * L
+
+F32 = mybir.dt.float32
+BF16 = mybir.dt.bfloat16
+I32 = mybir.dt.int32
+U32 = mybir.dt.uint32
+U16 = mybir.dt.uint16
+U8 = mybir.dt.uint8
+FP8X4 = mybir.dt.float8_e4m3fn_x4
+FP4X4 = mybir.dt.float4_e2m1fn_x4
+ACT = mybir.ActivationFunctionType
+ALU = mybir.AluOpType
+
+P = 128
+PACK = 4
+PASS = P * PACK
+PASSES = H // PASS
+BANK = 512
+RUN = 4
+
+
+def tile_list_sense_link_scores_kernel(
+    tc, tab_words, tab_scales, offs, pos1, pos2, w1, w2_words, w2_scales, w3, gain, shift, wt, rel, out
+):
+    nc = tc.nc
+    with ExitStack() as ctx:
+        lists = ctx.enter_context(tc.tile_pool(name="lists", bufs=1))
+        held = ctx.enter_context(tc.tile_pool(name="held", bufs=1))
+        ring = ctx.enter_context(tc.tile_pool(name="ring", bufs=2))
+        psum = ctx.enter_context(tc.psum_pool(name="psum", bufs=4))
+
+        offs_sb = lists.tile([P, S // 16], U16, name="offs_sb")
+        pos1_sb = lists.tile([P, L // 16], U16, name="pos1_sb")
+        pos2_sb = lists.tile([P, L // 16], U16, name="pos2_sb")
+
+        def load_weight(w, b, name):
+            raw = held.tile([P, PACK, PASS], F32, name=name, tag="staged")
+            nc.sync.dma_start(out=raw[:], in_=w.rearrange("(p j) c -> p j c", j=PACK)[:, :, b * PASS : (b + 1) * PASS])
+            return raw
+
+        def load_plane(queue, engine, scales, width, name):
+            plane = held.tile([P, width], U8, name=name, align_bytes=64)
+            engine.memset(plane[:].bitcast(I32), 0)
+            for r in range(4):
+                queue.dma_start(out=plane[r:P:32, :].bitcast(I32), in_=scales[0, r:16:4, :].bitcast(I32))
+            return plane
+
+        def load_channels(vec, name):
+            cols = held.tile([P, PASSES, PACK], F32, name=name)
+            nc.gpsimd.dma_start(out=cols[:], in_=vec.rearrange("(b p t) -> p b t", b=PASSES, t=PACK))
+            return cols
+
+        nc.sync.dma_start(offs_sb[:], offs)
+        w3_raw = load_weight(w3, 0, "w3_raw0")
+        tab_plane = load_plane(nc.sync, nc.vector, tab_scales, T, "tab_plane")
+        w2_plane = load_plane(nc.gpsimd, nc.gpsimd, w2_scales, H, "w2_plane")
+        tab_sb = held.tile([P, T], I32, name="tab_sb")
+        nc.sync.dma_start(out=tab_sb[:], in_=tab_words[0].rearrange("p t i -> p (t i)").bitcast(I32))
+        nc.sync.dma_start(pos2_sb[:], pos2)
+        w2_raw = held.tile([P, 2 * H], U8, name="w2_raw")
+        nc.sync.dma_start(out=w2_raw[:].bitcast(I32), in_=w2_words[0].bitcast(I32))
+        nc.sync.dma_start(pos1_sb[:], pos1)
+        gain_c = load_channels(gain, "gain_c")
+        shift_c = load_channels(shift, "shift_c")
+        wt_c = load_channels(wt, "wt_c")
+        gain_wt = held.tile([P, PASSES, PACK], F32, name="gain_wt")
+        shift_wt = held.tile([P, PASSES, PACK], F32, name="shift_wt")
+        nc.gpsimd.tensor_tensor(gain_wt[:], gain_c[:], wt_c[:], ALU.mult)
+        nc.gpsimd.tensor_tensor(shift_wt[:], shift_c[:], wt_c[:], ALU.mult)
+
+        def copy_on(engine, dst, src):
+            if engine == "vector":
+                nc.vector.tensor_copy(out=dst, in_=src)
+            elif engine == "gpsimd":
+                nc.gpsimd.tensor_scalar(dst, src, 1.0, 0.0, ALU.mult, ALU.add)
+            else:
+                nc.scalar.copy(out=dst, in_=src)
+
+        def quantise(grouped, width, name):
+            codes = held.tile([P, width], U32, name=name + "_codes", align_bytes=64)
+            plane = held.tile([P, width], U8, name=name + "_plane", align_bytes=64)
+            nc.vector.quantize_mx(out=codes[:].bitcast(FP8X4), scales=plane[:], in_=grouped[:])
+            return codes, plane
+
+        def weave_weight(engine, raw, name):
+            grouped = held.tile([P, PASS * PACK], BF16, name=name, align_bytes=64)
+            copy_on(
+                engine,
+                grouped[:].rearrange("p (t m j) -> p m j t", t=PACK, j=PACK),
+                raw[:].rearrange("p j (m t) -> p m j t", t=PACK),
+            )
+            return grouped
+
+        def weave_rows(engine, rows, name, width):
+            grouped = held.tile([P, width * PACK], BF16, name=name, align_bytes=64)
+            copy_on(
+                engine,
+                grouped[:].rearrange("p (c i t) -> p c t i", i=RUN, t=PACK),
+                rows[:].rearrange("p t (c i) -> p c t i", i=RUN),
+            )
+            return grouped
+
+        v_plane = held.tile([P, S], U8, name="v_plane", align_bytes=64)
+        nc.vector.tensor_copy(v_plane[:], tab_plane[:].indirect(offs_sb[:]))
+        w3_q = [quantise(weave_weight("scalar", w3_raw, "w3_g0"), PASS, "w3_q0")]
+        w1_raw = load_weight(w1, 0, "w1_raw0")
+        w2_dealt_plane = held.tile([P, H], U8, name="w2_dealt_plane", align_bytes=64)
+        nc.vector.tensor_copy(
+            out=w2_dealt_plane[:].rearrange("p (b t m) -> p b t m", b=PASSES, t=PACK),
+            in_=w2_plane[:].rearrange("p (b m t) -> p b t m", b=PASSES, t=PACK),
+        )
+        v_words = held.tile([P, S], U32, name="v_words", align_bytes=64)
+        for half in range(S // BANK):
+            nc.vector.tensor_copy(
+                v_words[:, half * BANK : (half + 1) * BANK],
+                tab_sb[:].bitcast(U32).indirect(offs_sb[:, half * BANK // 16 : (half + 1) * BANK // 16]),
+            )
+        w2_dealt = held.tile([P, 2 * H], U8, name="w2_dealt", align_bytes=64)
+        nc.vector.tensor_copy(
+            out=w2_dealt[:].bitcast(U16).rearrange("p (b t m) -> p b t m", b=PASSES, t=PACK),
+            in_=w2_raw[:].bitcast(U16).rearrange("p (b m t) -> p b t m", b=PASSES, t=PACK),
+        )
+        w1_q = [quantise(weave_weight("vector", w1_raw, "w1_g0"), PASS, "w1_q0")]
+
+        def first_stage(codes, plane, half, tag):
+            acc = psum.tile([P, BANK], F32, name=tag)
+            cols = slice(half * BANK, (half + 1) * BANK)
+            nc.tensor.matmul_mx(
+                out=acc[:], lhsT=codes, lhsT_scale=plane,
+                rhs=v_words[:, cols].bitcast(FP8X4), rhs_scale=v_plane[:, cols], start=True, stop=True,
+            )
+            return acc
+
+        STEPS = PASSES * PACK
+        views, bents, totals = {}, {}, {}
+        x1_rows, x2_rows, x3_rows = {}, {}, {}
+        x1_q, x2_q, x3_q = {}, {}, {}
+
+        def make_view(s):
+            b, t = divmod(s, PACK)
+            codes, plane = w3_q[b]
+            ch = slice(t * P, (t + 1) * P)
+            views[s] = ring.tile([P, S], F32, name="view", bufs=4)
+            for half in range(S // BANK):
+                acc = first_stage(codes[:, ch].bitcast(FP8X4), plane[:, ch], half, "bank_s")
+                nc.scalar.copy(out=views[s][:, half * BANK : (half + 1) * BANK], in_=acc[:])
+
+        def make_bent(s):
+            b, t = divmod(s, PACK)
+            codes, plane = w1_q[b]
+            ch = slice(t * P, (t + 1) * P)
+            bents[s] = ring.tile([P, S], F32, name="bent", bufs=3)
+            for half in range(S // BANK):
+                acc = first_stage(codes[:, ch].bitcast(FP8X4), plane[:, ch], half, "bank_s")
+                nc.scalar.activation(out=bents[s][:, half * BANK : (half + 1) * BANK], in_=acc[:], func=ACT.Tanh)
+
+        def make_total(s):
+            s0 = s * P
+            totals[s] = ring.tile([P, S], F32, name="total", bufs=3)
+            for half in range(S // BANK):
+                cols = slice(half * BANK, (half + 1) * BANK)
+                straight = first_stage(w2_dealt[:, 2 * s0 : 2 * (s0 + P)].bitcast(FP4X4), w2_dealt_plane[:, s0 : s0 + P], half, "bank_v")
+                nc.vector.tensor_tensor(totals[s][:, cols], straight[:], bents[s][:, cols], ALU.add)
+
+        def pick_x3(s):
+            b, t = divmod(s, PACK)
+            if t == 0:
+                x3_rows[b] = ring.tile([P, PACK, L], F32, name="x3_rows")
+            nc.vector.tensor_copy(x3_rows[b][:, t, :], views[s][:].indirect(pos2_sb[:]))
+
+        def pick_x2(s):
+            b, t = divmod(s, PACK)
+            if t == 0:
+                x2_rows[b] = ring.tile([P, PACK, L], BF16, name="x2_rows")
+            at_p2 = ring.tile([P, L], F32, name="at_p2", bufs=4)
+            nc.vector.tensor_copy(at_p2[:], totals[s][:].indirect(pos2_sb[:]))
+            return lambda: nc.scalar.activation(
+                out=x2_rows[b][:, t, :], in_=at_p2[:], func=ACT.Identity,
+                scale=gain_wt[:, b, t : t + 1], bias=shift_wt[:, b, t : t + 1],
+            )
+
+        def pick_x1(s, part, width):
+            b, t = divmod(s, PACK)
+            if t == 0:
+                x1_rows[b, part] = ring.tile([P, PACK, width], BF16, name="x1_rows", bufs=3)
+            at_p1 = ring.tile([P, width], F32, name="at_p1", bufs=4)
+            nc.vector.tensor_copy(at_p1[:], totals[s][:].indirect(pos1_sb[:, part * width // 16 : (part + 1) * width // 16]))
+            return lambda: nc.scalar.activation(out=x1_rows[b, part][:, t, :], in_=at_p1[:], func=ACT.Copy, scale=gain_c[:, b, t : t + 1])
+
+        def second_stage(rhs_q, mc, tag):
+            acc = psum.tile([P, BANK], F32, name=tag)
+            rows = slice(mc * P, (mc + 1) * P)
+            for b in range(PASSES):
+                nc.tensor.matmul_mx(
+                    out=acc[:], lhsT=x1_q[b][0][:, rows].bitcast(FP8X4), lhsT_scale=x1_q[b][1][:, rows],
+                    rhs=rhs_q[b][0][:].bitcast(FP8X4), rhs_scale=rhs_q[b][1][:], start=(b == 0), stop=(b == PASSES - 1),
+                )
+            return acc
+
+        for s in range(2):
+            make_view(s)
+            pick_x3(s)
+        make_bent(0)
+        later = []
+        for s in range(STEPS):
+            b, t = divmod(s, PACK)
+            if s + 2 < PACK:
+                make_view(s + 2)
+            if s + 1 < STEPS:
+                make_bent(s + 1)
+            make_total(s)
+            if s >= 6:
+                for u in range(PACK + (s - 6) * 2, min(STEPS, PACK + (s - 6 + 1) * 2)):
+                    make_view(u)
+            for f in later:
+                f()
+            later = [pick_x2(s), pick_x1(s, 0, L)]
+            if s + 2 < PACK:
+                pick_x3(s + 2)
+            if s == 0:
+                w1_q.append(quantise(weave_weight("scalar", load_weight(w1, 1, "w1_raw1"), "w1_g1"), PASS, "w1_q1"))
+            if s == 1:
+                w3_q.append(quantise(weave_weight("scalar", load_weight(w3, 1, "w3_raw1"), "w3_g1"), PASS, "w3_q1"))
+                rel_sb = held.tile([P, L], F32, name="rel_sb", tag="staged")
+                nc.sync.dma_start(out=rel_sb[:], in_=rel.partition_broadcast(P))
+            if s == 2:
+                x3_q[0] = quantise(weave_rows("scalar", x3_rows[0], "x3_g0", L), L, "x3_q0")
+            if s == 4:
+                x2_q[0] = quantise(weave_rows("scalar", x2_rows[0], "x2_g0", L), L, "x2_q0")
+            if s == 4:
+                x1_q[0] = quantise(weave_rows("scalar", x1_rows[0, 0], "x1_g0", L), L, "x1_q0")
+        for f in later:
+            f()
+        for s in range(PACK, STEPS):
+            pick_x3(s)
+        x1_q[1] = quantise(weave_rows("scalar", x1_rows[1, 0], "x1_g1", L), L, "x1_q1")
+        x2_q[1] = quantise(weave_rows("scalar", x2_rows[1], "x2_g1", L), L, "x2_q1")
+        x3_q[1] = quantise(weave_rows("vector", x3_rows[1], "x3_g1", L), L, "x3_q1")
+        for mc in range(L // P):
+            e_sb = ring.tile([P, L], F32, name="e_sb", bufs=4)
+            nc.scalar.copy(out=e_sb[:], in_=second_stage(x2_q, mc, "bank_s")[:])
+            larger = ring.tile([P, L], F32, name="larger")
+            nc.vector.tensor_tensor(larger[:], second_stage(x3_q, mc, "bank_v")[:], e_sb[:], ALU.max)
+            scored = ring.tile([P, L], F32, name="scored", bufs=4)
+            nc.vector.tensor_tensor(scored[:], larger[:], rel_sb[:], ALU.mult)
+            nc.sync.dma_start(out=out[mc * P : (mc + 1) * P, :], in_=scored[:])

@@ -20,8 +20,11 @@ P = 128
 PACK = 4
 PASS = P * PACK
 PASSES = H // PASS
+SLICES = PASSES * PACK
 BANK = 512
+HALVES = S // BANK
 RUN = 4
+PER_COLUMN = 16
 
 
 def tile_list_sense_link_scores_kernel(
@@ -31,101 +34,104 @@ def tile_list_sense_link_scores_kernel(
     with ExitStack() as ctx:
         lists = ctx.enter_context(tc.tile_pool(name="lists", bufs=1))
         held = ctx.enter_context(tc.tile_pool(name="held", bufs=1))
-        ring = ctx.enter_context(tc.tile_pool(name="ring", bufs=2))
+        staged = ctx.enter_context(tc.tile_pool(name="staged", bufs=1))
+        rows = ctx.enter_context(tc.tile_pool(name="rows", bufs=1))
+        ring = ctx.enter_context(tc.tile_pool(name="ring", bufs=4))
         psum = ctx.enter_context(tc.psum_pool(name="psum", bufs=4))
 
-        offs_sb = lists.tile([P, S // 16], U16, name="offs_sb")
-        pos1_sb = lists.tile([P, L // 16], U16, name="pos1_sb")
-        pos2_sb = lists.tile([P, L // 16], U16, name="pos2_sb")
+        def weight_pass(w, b):
+            return w.rearrange("(p j) c -> p j c", j=PACK)[:, :, b * PASS : (b + 1) * PASS]
 
-        def load_weight(w, b, name):
-            raw = held.tile([P, PACK, PASS], F32, name=name, tag="staged")
-            nc.sync.dma_start(out=raw[:], in_=w.rearrange("(p j) c -> p j c", j=PACK)[:, :, b * PASS : (b + 1) * PASS])
-            return raw
-
-        def load_plane(queue, engine, scales, width, name):
-            plane = held.tile([P, width], U8, name=name, align_bytes=64)
+        def load_scales(queue, engine, scales, width, name):
+            plane = held.tile([P, width], U8, name=name, tag=name, align_bytes=64)
             engine.memset(plane[:].bitcast(I32), 0)
             for r in range(4):
                 queue.dma_start(out=plane[r:P:32, :].bitcast(I32), in_=scales[0, r:16:4, :].bitcast(I32))
             return plane
 
-        def load_channels(vec, name):
-            cols = held.tile([P, PASSES, PACK], F32, name=name)
-            nc.gpsimd.dma_start(out=cols[:], in_=vec.rearrange("(b p t) -> p b t", b=PASSES, t=PACK))
-            return cols
-
-        nc.sync.dma_start(offs_sb[:], offs)
-        w3_raw = load_weight(w3, 0, "w3_raw0")
-        tab_plane = load_plane(nc.sync, nc.vector, tab_scales, T, "tab_plane")
-        w2_plane = load_plane(nc.gpsimd, nc.gpsimd, w2_scales, H, "w2_plane")
-        tab_sb = held.tile([P, T], I32, name="tab_sb")
-        nc.sync.dma_start(out=tab_sb[:], in_=tab_words[0].rearrange("p t i -> p (t i)").bitcast(I32))
-        nc.sync.dma_start(pos2_sb[:], pos2)
-        w2_raw = held.tile([P, 2 * H], U8, name="w2_raw")
-        nc.sync.dma_start(out=w2_raw[:].bitcast(I32), in_=w2_words[0].bitcast(I32))
-        nc.sync.dma_start(pos1_sb[:], pos1)
-        gain_c = load_channels(gain, "gain_c")
-        shift_c = load_channels(shift, "shift_c")
-        wt_c = load_channels(wt, "wt_c")
-        gain_wt = held.tile([P, PASSES, PACK], F32, name="gain_wt")
-        shift_wt = held.tile([P, PASSES, PACK], F32, name="shift_wt")
-        nc.gpsimd.tensor_tensor(gain_wt[:], gain_c[:], wt_c[:], ALU.mult)
-        nc.gpsimd.tensor_tensor(shift_wt[:], shift_c[:], wt_c[:], ALU.mult)
-
-        def copy_on(engine, dst, src):
-            if engine == "vector":
-                nc.vector.tensor_copy(out=dst, in_=src)
-            elif engine == "gpsimd":
-                nc.gpsimd.tensor_scalar(dst, src, 1.0, 0.0, ALU.mult, ALU.add)
-            else:
-                nc.scalar.copy(out=dst, in_=src)
-
         def quantise(grouped, width, name):
             codes = held.tile([P, width], U32, name=name + "_codes", align_bytes=64)
-            plane = held.tile([P, width], U8, name=name + "_plane", align_bytes=64)
+            plane = held.tile([P, width], U8, name=name + "_scales", align_bytes=64)
             nc.vector.quantize_mx(out=codes[:].bitcast(FP8X4), scales=plane[:], in_=grouped[:])
             return codes, plane
 
-        def weave_weight(engine, raw, name):
-            grouped = held.tile([P, PASS * PACK], BF16, name=name, align_bytes=64)
-            copy_on(
-                engine,
-                grouped[:].rearrange("p (t m j) -> p m j t", t=PACK, j=PACK),
-                raw[:].rearrange("p j (m t) -> p m j t", t=PACK),
+        def weave_weight(copy, grouped, raw, t0, t1):
+            copy(
+                out=grouped[:].rearrange("p (t m j) -> p m j t", t=t1 - t0, j=PACK),
+                in_=raw[:].rearrange("p j (m t) -> p m j t", t=PACK)[:, :, :, t0:t1],
             )
             return grouped
 
-        def weave_rows(engine, rows, name, width):
+        def weave_rows(copy, planes, width, name):
             grouped = held.tile([P, width * PACK], BF16, name=name, align_bytes=64)
-            copy_on(
-                engine,
-                grouped[:].rearrange("p (c i t) -> p c t i", i=RUN, t=PACK),
-                rows[:].rearrange("p t (c i) -> p c t i", i=RUN),
+            copy(
+                out=grouped[:].rearrange("p (c i t) -> p c t i", i=RUN, t=PACK),
+                in_=planes[:].rearrange("p t (c i) -> p c t i", i=RUN),
             )
             return grouped
 
-        v_plane = held.tile([P, S], U8, name="v_plane", align_bytes=64)
-        nc.vector.tensor_copy(v_plane[:], tab_plane[:].indirect(offs_sb[:]))
-        w3_q = [quantise(weave_weight("scalar", w3_raw, "w3_g0"), PASS, "w3_q0")]
-        w1_raw = load_weight(w1, 0, "w1_raw0")
-        w2_dealt_plane = held.tile([P, H], U8, name="w2_dealt_plane", align_bytes=64)
+        offs_sb = lists.tile([P, S // PER_COLUMN], U16, name="offs_sb")
+        pos1_sb = lists.tile([P, L // PER_COLUMN], U16, name="pos1_sb")
+        pos2_sb = lists.tile([P, L // PER_COLUMN], U16, name="pos2_sb")
+        nc.sync.dma_start(offs_sb[:], offs)
+        nc.sync.dma_start(pos2_sb[:], pos2)
+        nc.sync.dma_start(pos1_sb[:], pos1)
+        tab_plane = load_scales(nc.scalar, nc.vector, tab_scales, T, "tab_plane")
+        w2_plane = load_scales(nc.gpsimd, nc.gpsimd, w2_scales, H, "w2_plane")
+        w2_raw = held.tile([P, 2 * H], U8, name="w2_raw", tag="w1_raw")
+        nc.sync.dma_start(out=w2_raw[:].bitcast(I32), in_=w2_words[0].bitcast(I32))
+        tab_sb = staged.tile([P, T], I32, name="tab_sb", offset=0, align_bytes=64)
+        nc.sync.dma_start(out=tab_sb[:], in_=tab_words[0].rearrange("p t i -> p (t i)").bitcast(I32))
+
+        w2_codes = held.tile([P, 2 * H], U8, name="w2_codes", align_bytes=64)
         nc.vector.tensor_copy(
-            out=w2_dealt_plane[:].rearrange("p (b t m) -> p b t m", b=PASSES, t=PACK),
-            in_=w2_plane[:].rearrange("p (b m t) -> p b t m", b=PASSES, t=PACK),
-        )
-        v_words = held.tile([P, S], U32, name="v_words", align_bytes=64)
-        for half in range(S // BANK):
-            nc.vector.tensor_copy(
-                v_words[:, half * BANK : (half + 1) * BANK],
-                tab_sb[:].bitcast(U32).indirect(offs_sb[:, half * BANK // 16 : (half + 1) * BANK // 16]),
-            )
-        w2_dealt = held.tile([P, 2 * H], U8, name="w2_dealt", align_bytes=64)
-        nc.vector.tensor_copy(
-            out=w2_dealt[:].bitcast(U16).rearrange("p (b t m) -> p b t m", b=PASSES, t=PACK),
+            out=w2_codes[:].bitcast(U16).rearrange("p (b t m) -> p b t m", b=PASSES, t=PACK),
             in_=w2_raw[:].bitcast(U16).rearrange("p (b m t) -> p b t m", b=PASSES, t=PACK),
         )
-        w1_q = [quantise(weave_weight("vector", w1_raw, "w1_g0"), PASS, "w1_q0")]
+        w1_raw = held.tile([P, PACK, PASS], F32, name="w1_raw", tag="w1_raw")
+        nc.sync.dma_start(out=w1_raw[:], in_=weight_pass(w1, 0))
+        v_plane = held.tile([P, S], U8, name="v_plane", align_bytes=64)
+        nc.vector.tensor_copy(v_plane[:], tab_plane[:].indirect(offs_sb[:]))
+        channels = held.tile([P, 3, SLICES], F32, name="channels", tag="tab_plane", align_bytes=64)
+        for n, vec in enumerate((gain, shift, wt)):
+            nc.scalar.dma_start(
+                out=channels[:, n].rearrange("p (b t) -> p b t", t=PACK),
+                in_=vec.rearrange("(b p t) -> p b t", b=PASSES, t=PACK),
+            )
+        times_wt = held.tile([P, 2, SLICES], F32, name="times_wt")
+        for n in range(2):
+            nc.gpsimd.tensor_tensor(times_wt[:, n], channels[:, n], channels[:, 2], ALU.mult)
+        w2_scales_sb = held.tile([P, H], U8, name="w2_scales_sb", align_bytes=64)
+        nc.vector.tensor_copy(
+            out=w2_scales_sb[:].rearrange("p (b t m) -> p b t m", b=PASSES, t=PACK),
+            in_=w2_plane[:].rearrange("p (b m t) -> p b t m", b=PASSES, t=PACK),
+        )
+        v_words = held.tile([P, S], U32, name="v_words", tag="w2_plane", align_bytes=64)
+        for half in range(HALVES):
+            nc.vector.tensor_copy(
+                v_words[:, half * BANK : (half + 1) * BANK],
+                tab_sb[:].bitcast(U32).indirect(offs_sb[:, half * BANK // PER_COLUMN : (half + 1) * BANK // PER_COLUMN]),
+            )
+
+        w1_q, w3_q = {}, {}
+
+        def by_slice(store, quantised, s0, s1):
+            for s in range(s0, s1):
+                cols = slice((s - s0) * P, (s - s0 + 1) * P)
+                store[s] = (quantised[0][:, cols].bitcast(FP8X4), quantised[1][:, cols])
+
+        FIRST = 2
+        w1_first = staged.tile([P, FIRST * PASS], BF16, name="w1_first", offset=0, align_bytes=64)
+        w1_rest = staged.tile([P, (PACK - FIRST) * PASS], BF16, name="w1_rest", offset=4096, align_bytes=64)
+        weave_weight(nc.vector.tensor_copy, w1_first, w1_raw, 0, FIRST)
+        weave_weight(nc.scalar.copy, w1_rest, w1_raw, FIRST, PACK)
+        by_slice(w1_q, quantise(w1_first, FIRST * P, "w1_first"), 0, FIRST)
+
+        def later_weight(w, b, raw, store, name):
+            nc.sync.dma_start(out=raw[:], in_=weight_pass(w, b))
+            grouped = held.tile([P, PACK * PASS], BF16, name=name, align_bytes=64)
+            weave_weight(nc.scalar.copy, grouped, raw, 0, PACK)
+            by_slice(store, quantise(grouped, PASS, name), b * PACK, (b + 1) * PACK)
 
         def first_stage(codes, plane, half, tag):
             acc = psum.tile([P, BANK], F32, name=tag)
@@ -136,116 +142,114 @@ def tile_list_sense_link_scores_kernel(
             )
             return acc
 
-        STEPS = PASSES * PACK
-        views, bents, totals = {}, {}, {}
-        x1_rows, x2_rows, x3_rows = {}, {}, {}
+        views, bents = {}, {}
+        x1_planes, x2_planes, x3_planes = {}, {}, {}
         x1_q, x2_q, x3_q = {}, {}, {}
 
         def make_view(s):
-            b, t = divmod(s, PACK)
-            codes, plane = w3_q[b]
-            ch = slice(t * P, (t + 1) * P)
-            views[s] = ring.tile([P, S], F32, name="view", bufs=4)
-            for half in range(S // BANK):
-                acc = first_stage(codes[:, ch].bitcast(FP8X4), plane[:, ch], half, "bank_s")
+            views[s] = ring.tile([P, S], F32, name="view")
+            for half in range(HALVES):
+                acc = first_stage(*w3_q[s], half, "bank_scalar")
                 nc.scalar.copy(out=views[s][:, half * BANK : (half + 1) * BANK], in_=acc[:])
 
         def make_bent(s):
-            b, t = divmod(s, PACK)
-            codes, plane = w1_q[b]
-            ch = slice(t * P, (t + 1) * P)
-            bents[s] = ring.tile([P, S], F32, name="bent", bufs=3)
-            for half in range(S // BANK):
-                acc = first_stage(codes[:, ch].bitcast(FP8X4), plane[:, ch], half, "bank_s")
-                nc.scalar.activation(out=bents[s][:, half * BANK : (half + 1) * BANK], in_=acc[:], func=ACT.Tanh)
+            for half in range(HALVES):
+                acc = first_stage(*w1_q[s], half, "bank_scalar")
+                bents[s, half] = ring.tile([P, BANK], F32, name="bent", bufs=4)
+                nc.scalar.activation(out=bents[s, half][:], in_=acc[:], func=ACT.Tanh)
 
         def make_total(s):
-            s0 = s * P
-            totals[s] = ring.tile([P, S], F32, name="total", bufs=3)
-            for half in range(S // BANK):
-                cols = slice(half * BANK, (half + 1) * BANK)
-                straight = first_stage(w2_dealt[:, 2 * s0 : 2 * (s0 + P)].bitcast(FP4X4), w2_dealt_plane[:, s0 : s0 + P], half, "bank_v")
-                nc.vector.tensor_tensor(totals[s][:, cols], straight[:], bents[s][:, cols], ALU.add)
+            total = rows.tile([P, S], F32, name="total%d" % s, offset=2048)
+            for half in range(HALVES):
+                straight = first_stage(
+                    w2_codes[:, 2 * s * P : 2 * (s + 1) * P].bitcast(FP4X4), w2_scales_sb[:, s * P : (s + 1) * P], half, "bank_vector"
+                )
+                nc.vector.tensor_tensor(total[:, half * BANK : (half + 1) * BANK], straight[:], bents[s, half][:], ALU.add)
+            return total
 
-        def pick_x3(s):
+        def pick(total):
+            at_p2 = ring.tile([P, L], F32, name="at_p2")
+            nc.vector.tensor_copy(at_p2[:], total[:].indirect(pos2_sb[:]))
+            at_p1 = ring.tile([P, L], F32, name="at_p1")
+            nc.vector.tensor_copy(at_p1[:], total[:].indirect(pos1_sb[:]))
+            return at_p1, at_p2
+
+        def round_x2(s, at_p2):
             b, t = divmod(s, PACK)
             if t == 0:
-                x3_rows[b] = ring.tile([P, PACK, L], F32, name="x3_rows")
-            nc.vector.tensor_copy(x3_rows[b][:, t, :], views[s][:].indirect(pos2_sb[:]))
-
-        def pick_x2(s):
-            b, t = divmod(s, PACK)
-            if t == 0:
-                x2_rows[b] = ring.tile([P, PACK, L], BF16, name="x2_rows")
-            at_p2 = ring.tile([P, L], F32, name="at_p2", bufs=4)
-            nc.vector.tensor_copy(at_p2[:], totals[s][:].indirect(pos2_sb[:]))
-            return lambda: nc.scalar.activation(
-                out=x2_rows[b][:, t, :], in_=at_p2[:], func=ACT.Identity,
-                scale=gain_wt[:, b, t : t + 1], bias=shift_wt[:, b, t : t + 1],
+                x2_planes[b] = ring.tile([P, PACK, L], BF16, name="x2_planes", bufs=PASSES)
+            nc.scalar.activation(
+                out=x2_planes[b][:, t, :], in_=at_p2[:], func=ACT.Identity,
+                scale=times_wt[:, 0, s : s + 1], bias=times_wt[:, 1, s : s + 1],
             )
 
-        def pick_x1(s, part, width):
+        def round_x1(s, at_p1):
             b, t = divmod(s, PACK)
             if t == 0:
-                x1_rows[b, part] = ring.tile([P, PACK, width], BF16, name="x1_rows", bufs=3)
-            at_p1 = ring.tile([P, width], F32, name="at_p1", bufs=4)
-            nc.vector.tensor_copy(at_p1[:], totals[s][:].indirect(pos1_sb[:, part * width // 16 : (part + 1) * width // 16]))
-            return lambda: nc.scalar.activation(out=x1_rows[b, part][:, t, :], in_=at_p1[:], func=ACT.Copy, scale=gain_c[:, b, t : t + 1])
+                x1_planes[b] = ring.tile([P, PACK, L], BF16, name="x1_planes", bufs=PASSES)
+            nc.scalar.activation(out=x1_planes[b][:, t, :], in_=at_p1[:], func=ACT.Copy, scale=channels[:, 0, s : s + 1])
+
+        x3_planes[0] = held.tile([P, PACK, L], F32, name="x3_planes0")
+        make_bent(0)
+        by_slice(w1_q, quantise(w1_rest, (PACK - FIRST) * P, "w1_rest"), FIRST, PACK)
+        picked = {}
+        for s in range(SLICES):
+            if s + 1 < SLICES:
+                make_bent(s + 1)
+            total = make_total(s)
+            if 1 <= s <= PACK:
+                make_view(s - 1)
+            if s >= PACK:
+                make_view(s)
+            if s > 0:
+                round_x2(s - 1, picked[s - 1][1])
+                round_x1(s - 1, picked[s - 1][0])
+            picked[s] = pick(total)
+            if 2 <= s < 2 + PACK:
+                nc.vector.tensor_copy(x3_planes[0][:, s - 2, :], views[s - 2][:].indirect(pos2_sb[:]))
+            if s == 0:
+                later_weight(w3, 0, staged.tile([P, PACK, PASS], F32, name="w3_raw0", offset=8192, align_bytes=64), w3_q, "w3_0")
+            if s == 1:
+                later_weight(w1, 1, held.tile([P, PACK, PASS], F32, name="w1_raw1", tag="w1_raw"), w1_q, "w1_1")
+            if s == 2:
+                later_weight(w3, 1, staged.tile([P, PACK, PASS], F32, name="w3_raw1", offset=8192, align_bytes=64), w3_q, "w3_1")
+                rel_sb = staged.tile([P, L], F32, name="rel_sb", offset=0, align_bytes=64)
+                nc.sync.dma_start(out=rel_sb[:], in_=rel.partition_broadcast(P))
+            if s == 4:
+                x2_q[0] = quantise(weave_rows(nc.scalar.copy, x2_planes[0], L, "x2_0"), L, "x2_0")
+            if s == 5:
+                x1_q[0] = quantise(weave_rows(nc.scalar.copy, x1_planes[0], L, "x1_0"), L, "x1_0")
+            if s == 6:
+                x3_q[0] = quantise(weave_rows(nc.scalar.copy, x3_planes[0], L, "x3_0"), L, "x3_0")
+
+        last = SLICES - 1
+        round_x2(last, picked[last][1])
+        x2_g = weave_rows(nc.scalar.copy, x2_planes[1], L, "x2_1")
+        round_x1(last, picked[last][0])
+        x1_g = weave_rows(nc.scalar.copy, x1_planes[1], L, "x1_1")
+        x3_planes[1] = rows.tile([P, PACK, L], F32, name="x3_planes1", offset=0)
+        for t in range(PACK):
+            nc.vector.tensor_copy(x3_planes[1][:, t, :], views[PACK + t][:].indirect(pos2_sb[:]))
+        x3_g = weave_rows(nc.vector.tensor_copy, x3_planes[1], L, "x3_1")
+        x2_q[1] = quantise(x2_g, L, "x2_1")
+        x1_q[1] = quantise(x1_g, L, "x1_1")
+        x3_q[1] = quantise(x3_g, L, "x3_1")
 
         def second_stage(rhs_q, mc, tag):
             acc = psum.tile([P, BANK], F32, name=tag)
-            rows = slice(mc * P, (mc + 1) * P)
+            cols = slice(mc * P, (mc + 1) * P)
             for b in range(PASSES):
                 nc.tensor.matmul_mx(
-                    out=acc[:], lhsT=x1_q[b][0][:, rows].bitcast(FP8X4), lhsT_scale=x1_q[b][1][:, rows],
+                    out=acc[:], lhsT=x1_q[b][0][:, cols].bitcast(FP8X4), lhsT_scale=x1_q[b][1][:, cols],
                     rhs=rhs_q[b][0][:].bitcast(FP8X4), rhs_scale=rhs_q[b][1][:], start=(b == 0), stop=(b == PASSES - 1),
                 )
             return acc
 
-        for s in range(2):
-            make_view(s)
-            pick_x3(s)
-        make_bent(0)
-        later = []
-        for s in range(STEPS):
-            b, t = divmod(s, PACK)
-            if s + 2 < PACK:
-                make_view(s + 2)
-            if s + 1 < STEPS:
-                make_bent(s + 1)
-            make_total(s)
-            if s >= 6:
-                for u in range(PACK + (s - 6) * 2, min(STEPS, PACK + (s - 6 + 1) * 2)):
-                    make_view(u)
-            for f in later:
-                f()
-            later = [pick_x2(s), pick_x1(s, 0, L)]
-            if s + 2 < PACK:
-                pick_x3(s + 2)
-            if s == 0:
-                w1_q.append(quantise(weave_weight("scalar", load_weight(w1, 1, "w1_raw1"), "w1_g1"), PASS, "w1_q1"))
-            if s == 1:
-                w3_q.append(quantise(weave_weight("scalar", load_weight(w3, 1, "w3_raw1"), "w3_g1"), PASS, "w3_q1"))
-                rel_sb = held.tile([P, L], F32, name="rel_sb", tag="staged")
-                nc.sync.dma_start(out=rel_sb[:], in_=rel.partition_broadcast(P))
-            if s == 2:
-                x3_q[0] = quantise(weave_rows("scalar", x3_rows[0], "x3_g0", L), L, "x3_q0")
-            if s == 4:
-                x2_q[0] = quantise(weave_rows("scalar", x2_rows[0], "x2_g0", L), L, "x2_q0")
-            if s == 4:
-                x1_q[0] = quantise(weave_rows("scalar", x1_rows[0, 0], "x1_g0", L), L, "x1_q0")
-        for f in later:
-            f()
-        for s in range(PACK, STEPS):
-            pick_x3(s)
-        x1_q[1] = quantise(weave_rows("scalar", x1_rows[1, 0], "x1_g1", L), L, "x1_q1")
-        x2_q[1] = quantise(weave_rows("scalar", x2_rows[1], "x2_g1", L), L, "x2_q1")
-        x3_q[1] = quantise(weave_rows("vector", x3_rows[1], "x3_g1", L), L, "x3_q1")
         for mc in range(L // P):
-            e_sb = ring.tile([P, L], F32, name="e_sb", bufs=4)
-            nc.scalar.copy(out=e_sb[:], in_=second_stage(x2_q, mc, "bank_s")[:])
+            e_sb = ring.tile([P, L], F32, name="e_sb")
+            nc.scalar.copy(out=e_sb[:], in_=second_stage(x2_q, mc, "bank_scalar")[:])
             larger = ring.tile([P, L], F32, name="larger")
-            nc.vector.tensor_tensor(larger[:], second_stage(x3_q, mc, "bank_v")[:], e_sb[:], ALU.max)
-            scored = ring.tile([P, L], F32, name="scored", bufs=4)
+            nc.vector.tensor_tensor(larger[:], second_stage(x3_q, mc, "bank_vector")[:], e_sb[:], ALU.max)
+            scored = ring.tile([P, L], F32, name="scored")
             nc.vector.tensor_tensor(scored[:], larger[:], rel_sb[:], ALU.mult)
             nc.sync.dma_start(out=out[mc * P : (mc + 1) * P, :], in_=scored[:])

@@ -25,6 +25,8 @@ BANK = 512
 HALVES = S // BANK
 RUN = 4
 PER_COLUMN = 16
+QUADRANT = 32
+DEPTH = 3
 
 
 def tile_list_sense_link_scores_kernel(
@@ -35,106 +37,105 @@ def tile_list_sense_link_scores_kernel(
         lists = ctx.enter_context(tc.tile_pool(name="lists", bufs=1))
         held = ctx.enter_context(tc.tile_pool(name="held", bufs=1))
         staged = ctx.enter_context(tc.tile_pool(name="staged", bufs=1))
-        rows = ctx.enter_context(tc.tile_pool(name="rows", bufs=1))
+        early = ctx.enter_context(tc.tile_pool(name="early", bufs=1))
+        totals = ctx.enter_context(tc.tile_pool(name="totals", bufs=1))
+        slots = ctx.enter_context(tc.tile_pool(name="slots", bufs=1))
         ring = ctx.enter_context(tc.tile_pool(name="ring", bufs=4))
         psum = ctx.enter_context(tc.psum_pool(name="psum", bufs=4))
 
-        def weight_pass(w, b):
-            return w.rearrange("(p j) c -> p j c", j=PACK)[:, :, b * PASS : (b + 1) * PASS]
-
-        def load_scales(queue, engine, scales, width, name):
-            plane = held.tile([P, width], U8, name=name, tag=name, align_bytes=64)
-            engine.memset(plane[:].bitcast(I32), 0)
+        def load_scales(queue, plane, scales):
             for r in range(4):
-                queue.dma_start(out=plane[r:P:32, :].bitcast(I32), in_=scales[0, r:16:4, :].bitcast(I32))
-            return plane
+                queue.dma_start(out=plane[r:P:QUADRANT, :].bitcast(I32), in_=scales[0, r:16:4, :].bitcast(I32))
 
-        def quantise(grouped, width, name):
-            codes = held.tile([P, width], U32, name=name + "_codes", align_bytes=64)
-            plane = held.tile([P, width], U8, name=name + "_scales", align_bytes=64)
-            nc.vector.quantize_mx(out=codes[:].bitcast(FP8X4), scales=plane[:], in_=grouped[:])
+        def load_weight(w, b, name, offset):
+            raw = staged.tile([P, PACK, PASS], F32, name=name, offset=offset, align_bytes=64)
+            nc.sync.dma_start(out=raw[:], in_=w.rearrange("(p j) c -> p j c", j=PACK)[:, :, b * PASS : (b + 1) * PASS])
+            return raw
+
+        def weave_weight(copy, raw, grouped):
+            copy(
+                out=grouped[:].rearrange("p (t g e j) -> p g t j e", t=PACK, e=RUN, j=PACK),
+                in_=raw[:].rearrange("p j (g t e) -> p g t j e", t=PACK, e=RUN),
+            )
+            return grouped
+
+        def weave_rows(copy, planes, grouped, c0, c1):
+            copy(
+                out=grouped[:, c0 * PACK : c1 * PACK].rearrange("p (c i t) -> p c t i", i=RUN, t=PACK),
+                in_=planes[:, :, c0:c1].rearrange("p t (c i) -> p c t i", i=RUN),
+            )
+
+        def operand(name):
+            codes = held.tile([P, L], U32, name=name + "_codes", align_bytes=64)
+            plane = held.tile([P, L], U8, name=name + "_scales", align_bytes=64)
             return codes, plane
 
-        def weave_weight(copy, grouped, raw, t0, t1):
-            copy(
-                out=grouped[:].rearrange("p (t m j) -> p m j t", t=t1 - t0, j=PACK),
-                in_=raw[:].rearrange("p j (m t) -> p m j t", t=PACK)[:, :, :, t0:t1],
+        def quantise(target, grouped, c0, c1):
+            nc.vector.quantize_mx(
+                out=target[0][:, c0:c1].bitcast(FP8X4), scales=target[1][:, c0:c1], in_=grouped[:, c0 * PACK : c1 * PACK]
             )
-            return grouped
-
-        def weave_rows(copy, planes, width, name):
-            grouped = held.tile([P, width * PACK], BF16, name=name, align_bytes=64)
-            copy(
-                out=grouped[:].rearrange("p (c i t) -> p c t i", i=RUN, t=PACK),
-                in_=planes[:].rearrange("p t (c i) -> p c t i", i=RUN),
-            )
-            return grouped
 
         offs_sb = lists.tile([P, S // PER_COLUMN], U16, name="offs_sb")
         pos1_sb = lists.tile([P, L // PER_COLUMN], U16, name="pos1_sb")
         pos2_sb = lists.tile([P, L // PER_COLUMN], U16, name="pos2_sb")
         nc.sync.dma_start(offs_sb[:], offs)
-        nc.sync.dma_start(pos2_sb[:], pos2)
         nc.sync.dma_start(pos1_sb[:], pos1)
-        tab_plane = load_scales(nc.scalar, nc.vector, tab_scales, T, "tab_plane")
-        w2_plane = load_scales(nc.gpsimd, nc.gpsimd, w2_scales, H, "w2_plane")
-        w2_raw = held.tile([P, 2 * H], U8, name="w2_raw", tag="w1_raw")
+        nc.sync.dma_start(pos2_sb[:], pos2)
+        tab_plane = early.tile([P, T], U8, name="tab_plane", offset=2 * PACK * PASS + H, align_bytes=64)
+        nc.vector.memset(tab_plane[:].bitcast(I32), 0)
+        load_scales(nc.scalar, tab_plane, tab_scales)
+        w2_plane = early.tile([P, H], U8, name="w2_plane", offset=2 * PACK * PASS, align_bytes=64)
+        nc.gpsimd.memset(w2_plane[:].bitcast(I32), 0)
+        load_scales(nc.gpsimd, w2_plane, w2_scales)
+        w2_raw = held.tile([P, 2 * H], U8, name="w2_raw")
         nc.sync.dma_start(out=w2_raw[:].bitcast(I32), in_=w2_words[0].bitcast(I32))
+        w1_raw = load_weight(w1, 0, "w1_raw0", 4 * T)
         tab_sb = staged.tile([P, T], I32, name="tab_sb", offset=0, align_bytes=64)
         nc.sync.dma_start(out=tab_sb[:], in_=tab_words[0].rearrange("p t i -> p (t i)").bitcast(I32))
+        vec_rows = held.tile([P, PASSES, P], F32, name="vec_rows")
+        nc.vector.memset(vec_rows[:], 0.0)
+        for n, vec in enumerate((gain, shift, wt)):
+            nc.gpsimd.dma_start(out=vec_rows[n:P:QUADRANT], in_=vec.rearrange("(b q x) -> q b x", b=PASSES, x=P))
 
         w2_codes = held.tile([P, 2 * H], U8, name="w2_codes", align_bytes=64)
         nc.vector.tensor_copy(
-            out=w2_codes[:].bitcast(U16).rearrange("p (b t m) -> p b t m", b=PASSES, t=PACK),
-            in_=w2_raw[:].bitcast(U16).rearrange("p (b m t) -> p b t m", b=PASSES, t=PACK),
+            out=w2_codes[:].bitcast(I32).rearrange("p (b t g w) -> p b t g w", b=PASSES, t=PACK, w=2),
+            in_=w2_raw[:].bitcast(I32).rearrange("p (b g t w) -> p b t g w", b=PASSES, t=PACK, w=2),
         )
-        w1_raw = held.tile([P, PACK, PASS], F32, name="w1_raw", tag="w1_raw")
-        nc.sync.dma_start(out=w1_raw[:], in_=weight_pass(w1, 0))
         v_plane = held.tile([P, S], U8, name="v_plane", align_bytes=64)
         nc.vector.tensor_copy(v_plane[:], tab_plane[:].indirect(offs_sb[:]))
-        channels = held.tile([P, 3, SLICES], F32, name="channels", tag="tab_plane", align_bytes=64)
-        for n, vec in enumerate((gain, shift, wt)):
-            nc.scalar.dma_start(
-                out=channels[:, n].rearrange("p (b t) -> p b t", t=PACK),
-                in_=vec.rearrange("(b p t) -> p b t", b=PASSES, t=PACK),
-            )
-        times_wt = held.tile([P, 2, SLICES], F32, name="times_wt")
-        for n in range(2):
-            nc.gpsimd.tensor_tensor(times_wt[:, n], channels[:, n], channels[:, 2], ALU.mult)
         w2_scales_sb = held.tile([P, H], U8, name="w2_scales_sb", align_bytes=64)
         nc.vector.tensor_copy(
-            out=w2_scales_sb[:].rearrange("p (b t m) -> p b t m", b=PASSES, t=PACK),
-            in_=w2_plane[:].rearrange("p (b m t) -> p b t m", b=PASSES, t=PACK),
+            out=w2_scales_sb[:].bitcast(I32).rearrange("p (b t g) -> p b t g", b=PASSES, t=PACK),
+            in_=w2_plane[:].bitcast(I32).rearrange("p (b g t) -> p b t g", b=PASSES, t=PACK),
         )
-        v_words = held.tile([P, S], U32, name="v_words", tag="w2_plane", align_bytes=64)
+        w1_q, w3_q = {}, {}
+        w1_q[0] = (
+            early.tile([P, PASS], U32, name="w1_0_codes", offset=2 * PACK * PASS + H, align_bytes=64),
+            held.tile([P, PASS], U8, name="w1_0_scales", align_bytes=64),
+        )
+        quantise(w1_q[0], weave_weight(nc.scalar.copy, w1_raw, early.tile([P, PACK * PASS], BF16, name="w1_0", offset=0, align_bytes=64)), 0, PASS)
+        v_words = early.tile([P, S], U32, name="v_words", offset=H, align_bytes=64)
         for half in range(HALVES):
             nc.vector.tensor_copy(
                 v_words[:, half * BANK : (half + 1) * BANK],
                 tab_sb[:].bitcast(U32).indirect(offs_sb[:, half * BANK // PER_COLUMN : (half + 1) * BANK // PER_COLUMN]),
             )
 
-        w1_q, w3_q = {}, {}
-
-        def by_slice(store, quantised, s0, s1):
-            for s in range(s0, s1):
-                cols = slice((s - s0) * P, (s - s0 + 1) * P)
-                store[s] = (quantised[0][:, cols].bitcast(FP8X4), quantised[1][:, cols])
-
-        FIRST = 2
-        w1_first = staged.tile([P, FIRST * PASS], BF16, name="w1_first", offset=0, align_bytes=64)
-        w1_rest = staged.tile([P, (PACK - FIRST) * PASS], BF16, name="w1_rest", offset=4096, align_bytes=64)
-        weave_weight(nc.vector.tensor_copy, w1_first, w1_raw, 0, FIRST)
-        weave_weight(nc.scalar.copy, w1_rest, w1_raw, FIRST, PACK)
-        by_slice(w1_q, quantise(w1_first, FIRST * P, "w1_first"), 0, FIRST)
-
-        def later_weight(w, b, raw, store, name):
-            nc.sync.dma_start(out=raw[:], in_=weight_pass(w, b))
-            grouped = held.tile([P, PACK * PASS], BF16, name=name, align_bytes=64)
-            weave_weight(nc.scalar.copy, grouped, raw, 0, PACK)
-            by_slice(store, quantise(grouped, PASS, name), b * PACK, (b + 1) * PACK)
+        vec_dealt = held.tile([P, SLICES * QUADRANT], F32, name="vec_dealt", align_bytes=64)
+        nc.gpsimd.tensor_copy(
+            out=vec_dealt[:].rearrange("p (b t g e) -> p b t g e", b=PASSES, t=PACK, e=RUN),
+            in_=vec_rows[:].rearrange("p b (g t e) -> p b t g e", t=PACK, e=RUN),
+        )
+        channels = early.tile([P, SLICES * QUADRANT], F32, name="channels", offset=0, align_bytes=64)
+        nc.vector.transpose(channels[:], vec_dealt[:])
+        by_slice = channels[:].rearrange("p (s n) -> p n s", n=QUADRANT)
+        times_wt = held.tile([P, 2, SLICES], F32, name="times_wt")
+        for n in range(2):
+            nc.gpsimd.tensor_tensor(times_wt[:, n], by_slice[:, n], by_slice[:, 2], ALU.mult)
 
         def first_stage(codes, plane, half, tag):
-            acc = psum.tile([P, BANK], F32, name=tag)
+            acc = psum.tile([P, BANK], F32, name=tag, bufs=4 if tag == "bank_scalar" else 4)
             cols = slice(half * BANK, (half + 1) * BANK)
             nc.tensor.matmul_mx(
                 out=acc[:], lhsT=codes, lhsT_scale=plane,
@@ -142,101 +143,155 @@ def tile_list_sense_link_scores_kernel(
             )
             return acc
 
-        views, bents = {}, {}
-        x1_planes, x2_planes, x3_planes = {}, {}, {}
+        def columns(quantised, s):
+            b, t = divmod(s, PACK)
+            return quantised[b][0][:, t * P : (t + 1) * P].bitcast(FP8X4), quantised[b][1][:, t * P : (t + 1) * P]
+
+        def slot(s, half, name):
+            return slots.tile([P, BANK], F32, name="%s%d_%d" % (name, s, half), offset=((s % DEPTH) * HALVES + half) * 4 * BANK)
+
+        views, bents, sums, picked = {}, {}, {}, {}
+        x1_planes = [held.tile([P, PACK, L], BF16, name="x1_planes%d" % b) for b in range(PASSES)]
+        x2_planes = [held.tile([P, PACK, L], BF16, name="x2_planes%d" % b) for b in range(PASSES)]
+        x3_planes = {}
         x1_q, x2_q, x3_q = {}, {}, {}
 
         def make_view(s):
-            views[s] = ring.tile([P, S], F32, name="view")
+            views[s] = ring.tile([P, S], F32, name="view", bufs=5)
             for half in range(HALVES):
-                acc = first_stage(*w3_q[s], half, "bank_scalar")
+                acc = first_stage(*columns(w3_q, s), half, "bank_scalar")
                 nc.scalar.copy(out=views[s][:, half * BANK : (half + 1) * BANK], in_=acc[:])
 
-        def make_bent(s):
-            for half in range(HALVES):
-                acc = first_stage(*w1_q[s], half, "bank_scalar")
-                bents[s, half] = ring.tile([P, BANK], F32, name="bent", bufs=4)
+        def make_bent(s, halves=range(HALVES)):
+            for half in halves:
+                acc = first_stage(*columns(w1_q, s), half, "bank_scalar")
+                bents[s, half] = slot(s, half, "bent")
                 nc.scalar.activation(out=bents[s, half][:], in_=acc[:], func=ACT.Tanh)
 
-        def make_total(s):
-            total = rows.tile([P, S], F32, name="total%d" % s, offset=2048)
-            for half in range(HALVES):
+        def make_sum(s, halves=range(HALVES)):
+            if s not in sums:
+                sums[s] = totals.tile([P, S], F32, name="sum%d" % s, offset=(1 + s % DEPTH) * 4 * S)
+            for half in halves:
                 straight = first_stage(
                     w2_codes[:, 2 * s * P : 2 * (s + 1) * P].bitcast(FP4X4), w2_scales_sb[:, s * P : (s + 1) * P], half, "bank_vector"
                 )
-                nc.vector.tensor_tensor(total[:, half * BANK : (half + 1) * BANK], straight[:], bents[s, half][:], ALU.add)
-            return total
+                nc.vector.tensor_tensor(sums[s][:, half * BANK : (half + 1) * BANK], straight[:], bents[s, half][:], ALU.add)
 
-        def pick(total):
-            at_p2 = ring.tile([P, L], F32, name="at_p2")
-            nc.vector.tensor_copy(at_p2[:], total[:].indirect(pos2_sb[:]))
-            at_p1 = ring.tile([P, L], F32, name="at_p1")
-            nc.vector.tensor_copy(at_p1[:], total[:].indirect(pos1_sb[:]))
-            return at_p1, at_p2
+        def pick(s):
+            for n, pos_sb in enumerate((pos1_sb, pos2_sb)):
+                picked[s, n] = slot(s + 1, n, "picked")
+                nc.vector.tensor_copy(picked[s, n][:], sums[s][:].indirect(pos_sb[:]))
 
-        def round_x2(s, at_p2):
+        def pick_view(s):
             b, t = divmod(s, PACK)
-            if t == 0:
-                x2_planes[b] = ring.tile([P, PACK, L], BF16, name="x2_planes", bufs=PASSES)
+            nc.vector.tensor_copy(x3_planes[b][:, t, :], views[s][:].indirect(pos2_sb[:]))
+
+        def round_x2(s):
+            b, t = divmod(s, PACK)
             nc.scalar.activation(
-                out=x2_planes[b][:, t, :], in_=at_p2[:], func=ACT.Identity,
+                out=x2_planes[b][:, t, :], in_=picked[s, 1][:], func=ACT.Identity,
                 scale=times_wt[:, 0, s : s + 1], bias=times_wt[:, 1, s : s + 1],
             )
 
-        def round_x1(s, at_p1):
+        def round_x1(s):
             b, t = divmod(s, PACK)
-            if t == 0:
-                x1_planes[b] = ring.tile([P, PACK, L], BF16, name="x1_planes", bufs=PASSES)
-            nc.scalar.activation(out=x1_planes[b][:, t, :], in_=at_p1[:], func=ACT.Copy, scale=channels[:, 0, s : s + 1])
+            nc.scalar.activation(out=x1_planes[b][:, t, :], in_=picked[s, 0][:], func=ACT.Copy, scale=channels[:, QUADRANT * s : QUADRANT * s + 1])
+
+        def later_weight(copy, raw, store, b, name):
+            store[b] = operand(name)
+            quantise(store[b], weave_weight(copy, raw, held.tile([P, PACK * PASS], BF16, name=name, align_bytes=64)), 0, PASS)
+
+        def rows_operand(copy, planes, store, b, name, parts=1):
+            grouped = held.tile([P, L * PACK], BF16, name=name, align_bytes=64)
+            store[b] = operand(name)
+            for part in range(parts):
+                weave_rows(copy, planes, grouped, part * L // parts, (part + 1) * L // parts)
+            for part in range(parts):
+                quantise(store[b], grouped, part * L // parts, (part + 1) * L // parts)
+
+        def rows_part(copy, planes, target, grouped, c0, c1):
+            weave_rows(copy, planes, grouped, c0, c1)
+            quantise(target, grouped, c0, c1)
 
         x3_planes[0] = held.tile([P, PACK, L], F32, name="x3_planes0")
-        make_bent(0)
-        by_slice(w1_q, quantise(w1_rest, (PACK - FIRST) * P, "w1_rest"), FIRST, PACK)
-        picked = {}
-        for s in range(SLICES):
-            if s + 1 < SLICES:
-                make_bent(s + 1)
-            total = make_total(s)
-            if 1 <= s <= PACK:
-                make_view(s - 1)
-            if s >= PACK:
-                make_view(s)
-            if s > 0:
-                round_x2(s - 1, picked[s - 1][1])
-                round_x1(s - 1, picked[s - 1][0])
-            picked[s] = pick(total)
-            if 2 <= s < 2 + PACK:
-                nc.vector.tensor_copy(x3_planes[0][:, s - 2, :], views[s - 2][:].indirect(pos2_sb[:]))
-            if s == 0:
-                later_weight(w3, 0, staged.tile([P, PACK, PASS], F32, name="w3_raw0", offset=8192, align_bytes=64), w3_q, "w3_0")
-            if s == 1:
-                later_weight(w1, 1, held.tile([P, PACK, PASS], F32, name="w1_raw1", tag="w1_raw"), w1_q, "w1_1")
-            if s == 2:
-                later_weight(w3, 1, staged.tile([P, PACK, PASS], F32, name="w3_raw1", offset=8192, align_bytes=64), w3_q, "w3_1")
-                rel_sb = staged.tile([P, L], F32, name="rel_sb", offset=0, align_bytes=64)
-                nc.sync.dma_start(out=rel_sb[:], in_=rel.partition_broadcast(P))
-            if s == 4:
-                x2_q[0] = quantise(weave_rows(nc.scalar.copy, x2_planes[0], L, "x2_0"), L, "x2_0")
-            if s == 5:
-                x1_q[0] = quantise(weave_rows(nc.scalar.copy, x1_planes[0], L, "x1_0"), L, "x1_0")
-            if s == 6:
-                x3_q[0] = quantise(weave_rows(nc.scalar.copy, x3_planes[0], L, "x3_0"), L, "x3_0")
-
-        last = SLICES - 1
-        round_x2(last, picked[last][1])
-        x2_g = weave_rows(nc.scalar.copy, x2_planes[1], L, "x2_1")
-        round_x1(last, picked[last][0])
-        x1_g = weave_rows(nc.scalar.copy, x1_planes[1], L, "x1_1")
-        x3_planes[1] = rows.tile([P, PACK, L], F32, name="x3_planes1", offset=0)
-        for t in range(PACK):
-            nc.vector.tensor_copy(x3_planes[1][:, t, :], views[PACK + t][:].indirect(pos2_sb[:]))
-        x3_g = weave_rows(nc.vector.tensor_copy, x3_planes[1], L, "x3_1")
-        x2_q[1] = quantise(x2_g, L, "x2_1")
-        x1_q[1] = quantise(x1_g, L, "x1_1")
-        x3_q[1] = quantise(x3_g, L, "x3_1")
+        make_bent(0, [0])
+        make_bent(1, [0])
+        make_sum(0, [0])
+        make_bent(0, [1])
+        make_sum(1, [0])
+        make_bent(1, [1])
+        make_sum(0, [1])
+        make_sum(1, [1])
+        make_bent(2)
+        pick(0)
+        make_bent(3)
+        make_sum(2)
+        later_weight(nc.scalar.copy, load_weight(w1, 1, "w1_raw1", 0), w1_q, 1, "w1_1")
+        pick(1)
+        round_x1(0)
+        round_x2(0)
+        later_weight(nc.scalar.copy, load_weight(w3, 0, "w3_raw0", 8192), w3_q, 0, "w3_0")
+        make_sum(3)
+        pick(2)
+        round_x1(1)
+        round_x2(1)
+        make_bent(4)
+        make_bent(5)
+        make_sum(4)
+        pick(3)
+        make_view(0)
+        later_weight(nc.scalar.copy, load_weight(w3, 1, "w3_raw1", 0), w3_q, 1, "w3_1")
+        round_x1(2)
+        round_x2(2)
+        make_bent(6)
+        make_sum(5)
+        pick(4)
+        make_view(1)
+        pick_view(0)
+        pick_view(1)
+        round_x1(3)
+        round_x2(3)
+        make_bent(7)
+        make_sum(6)
+        rows_operand(nc.vector.tensor_copy, x2_planes[0], x2_q, 0, "x2_0", 2)
+        pick(5)
+        make_view(2)
+        make_view(3)
+        pick_view(2)
+        pick_view(3)
+        round_x1(4)
+        round_x2(4)
+        make_sum(7)
+        pick(6)
+        pick(7)
+        rel_sb = staged.tile([P, L], F32, name="rel_sb", offset=0, align_bytes=64)
+        nc.sync.dma_start(out=rel_sb[:], in_=rel.partition_broadcast(P))
+        make_view(4)
+        make_view(5)
+        round_x1(5)
+        round_x2(5)
+        make_view(6)
+        rows_operand(nc.scalar.copy, x1_planes[0], x1_q, 0, "x1_0")
+        rows_operand(nc.scalar.copy, x3_planes[0], x3_q, 0, "x3_0")
+        make_view(7)
+        round_x1(6)
+        round_x2(6)
+        round_x1(7)
+        x1_q[1] = operand("x1_1")
+        x1_last = held.tile([P, L * PACK], BF16, name="x1_1", align_bytes=64)
+        rows_part(nc.scalar.copy, x1_planes[1], x1_q[1], x1_last, 0, L // 2)
+        round_x2(7)
+        rows_operand(nc.scalar.copy, x2_planes[1], x2_q, 1, "x2_1")
+        rows_part(nc.scalar.copy, x1_planes[1], x1_q[1], x1_last, L // 2, L)
+        x3_planes[1] = totals.tile([P, PACK, L], F32, name="x3_planes1", offset=0)
+        pick_view(4)
+        pick_view(5)
+        pick_view(6)
+        pick_view(7)
+        rows_operand(nc.vector.tensor_copy, x3_planes[1], x3_q, 1, "x3_1", 2)
 
         def second_stage(rhs_q, mc, tag):
-            acc = psum.tile([P, BANK], F32, name=tag)
+            acc = psum.tile([P, BANK], F32, name=tag, bufs=4 if tag == "bank_scalar" else 4)
             cols = slice(mc * P, (mc + 1) * P)
             for b in range(PASSES):
                 nc.tensor.matmul_mx(
@@ -245,11 +300,13 @@ def tile_list_sense_link_scores_kernel(
                 )
             return acc
 
+        e_sb = {}
         for mc in range(L // P):
-            e_sb = ring.tile([P, L], F32, name="e_sb")
-            nc.scalar.copy(out=e_sb[:], in_=second_stage(x2_q, mc, "bank_scalar")[:])
+            e_sb[mc] = ring.tile([P, L], F32, name="e_sb")
+            nc.scalar.copy(out=e_sb[mc][:], in_=second_stage(x3_q, mc, "bank_scalar")[:])
+        for mc in range(L // P):
             larger = ring.tile([P, L], F32, name="larger")
-            nc.vector.tensor_tensor(larger[:], second_stage(x3_q, mc, "bank_vector")[:], e_sb[:], ALU.max)
+            nc.vector.tensor_tensor(larger[:], second_stage(x2_q, mc, "bank_vector")[:], e_sb[mc][:], ALU.max)
             scored = ring.tile([P, L], F32, name="scored")
-            nc.vector.tensor_tensor(scored[:], larger[:], rel_sb[:], ALU.mult)
+            (nc.gpsimd if mc < 0 else nc.vector).tensor_tensor(scored[:], larger[:], rel_sb[:], ALU.mult)
             nc.sync.dma_start(out=out[mc * P : (mc + 1) * P, :], in_=scored[:])

@@ -26,7 +26,17 @@ HALVES = S // BANK
 RUN = 4
 PER_COLUMN = 16
 QUADRANT = 32
+SCALE_ROWS = 4
 DEPTH = 3
+VIEW_BUFS = 5
+CHUNKS = L // P
+
+FIRST_WEIGHT_AT = 4 * T
+W2_SCALES_AT = 0
+VECTORS_AT = H
+WEIGHT_A_AT = 2 * H
+WEIGHT_B_AT = WEIGHT_A_AT + 4 * PACK * PASS
+TAB_SCALES_AT = 2 * PACK * PASS
 
 
 def tile_list_sense_link_scores_kernel(
@@ -37,38 +47,34 @@ def tile_list_sense_link_scores_kernel(
         lists = ctx.enter_context(tc.tile_pool(name="lists", bufs=1))
         held = ctx.enter_context(tc.tile_pool(name="held", bufs=1))
         staged = ctx.enter_context(tc.tile_pool(name="staged", bufs=1))
+        tail = ctx.enter_context(tc.tile_pool(name="tail", bufs=1))
         early = ctx.enter_context(tc.tile_pool(name="early", bufs=1))
         totals = ctx.enter_context(tc.tile_pool(name="totals", bufs=1))
         slots = ctx.enter_context(tc.tile_pool(name="slots", bufs=1))
-        ring = ctx.enter_context(tc.tile_pool(name="ring", bufs=4))
+        ring = ctx.enter_context(tc.tile_pool(name="ring", bufs=CHUNKS))
         psum = ctx.enter_context(tc.psum_pool(name="psum", bufs=4))
-
-        def load_scales(queue, plane, scales):
-            for r in range(4):
-                queue.dma_start(out=plane[r:P:QUADRANT, :].bitcast(I32), in_=scales[0, r:16:4, :].bitcast(I32))
 
         def load_weight(w, b, name, offset):
             raw = staged.tile([P, PACK, PASS], F32, name=name, offset=offset, align_bytes=64)
             nc.sync.dma_start(out=raw[:], in_=w.rearrange("(p j) c -> p j c", j=PACK)[:, :, b * PASS : (b + 1) * PASS])
             return raw
 
-        def weave_weight(copy, raw, grouped):
-            copy(
+        def weave_weight(raw, grouped):
+            nc.scalar.copy(
                 out=grouped[:].rearrange("p (t g e j) -> p g t j e", t=PACK, e=RUN, j=PACK),
                 in_=raw[:].rearrange("p j (g t e) -> p g t j e", t=PACK, e=RUN),
             )
-            return grouped
 
-        def weave_rows(copy, planes, grouped, c0, c1):
+        def weave_rows(copy, by_slice_rows, grouped, c0, c1):
             copy(
                 out=grouped[:, c0 * PACK : c1 * PACK].rearrange("p (c i t) -> p c t i", i=RUN, t=PACK),
-                in_=planes[:, :, c0:c1].rearrange("p t (c i) -> p c t i", i=RUN),
+                in_=by_slice_rows[:, :, c0:c1].rearrange("p t (c i) -> p c t i", i=RUN),
             )
 
         def operand(name):
             codes = held.tile([P, L], U32, name=name + "_codes", align_bytes=64)
-            plane = held.tile([P, L], U8, name=name + "_scales", align_bytes=64)
-            return codes, plane
+            scales = held.tile([P, L], U8, name=name + "_scales", align_bytes=64)
+            return codes, scales
 
         def quantise(target, grouped, c0, c1):
             nc.vector.quantize_mx(
@@ -79,21 +85,32 @@ def tile_list_sense_link_scores_kernel(
         pos1_sb = lists.tile([P, L // PER_COLUMN], U16, name="pos1_sb")
         pos2_sb = lists.tile([P, L // PER_COLUMN], U16, name="pos2_sb")
         nc.sync.dma_start(offs_sb[:], offs)
-        nc.sync.dma_start(pos1_sb[:], pos1)
-        nc.sync.dma_start(pos2_sb[:], pos2)
-        tab_plane = early.tile([P, T], U8, name="tab_plane", offset=2 * PACK * PASS + H, align_bytes=64)
-        nc.vector.memset(tab_plane[:].bitcast(I32), 0)
-        load_scales(nc.scalar, tab_plane, tab_scales)
-        w2_plane = early.tile([P, H], U8, name="w2_plane", offset=2 * PACK * PASS, align_bytes=64)
-        nc.gpsimd.memset(w2_plane[:].bitcast(I32), 0)
-        load_scales(nc.gpsimd, w2_plane, w2_scales)
+        tab_rows = held.tile([P, T // 4], I32, name="tab_rows")
+        for q in range(P // QUADRANT):
+            nc.sync.dma_start(
+                out=tab_rows[QUADRANT * q : QUADRANT * q + SCALE_ROWS, :],
+                in_=tab_scales[0, SCALE_ROWS * q : SCALE_ROWS * (q + 1), :].bitcast(I32),
+            )
+        tab_scales_sb = early.tile([P, T], U8, name="tab_scales_sb", offset=TAB_SCALES_AT, align_bytes=64)
+        nc.vector.memset(tab_scales_sb[:].bitcast(I32), 0)
+        for q in range(P // QUADRANT):
+            live = slice(QUADRANT * q, QUADRANT * q + SCALE_ROWS)
+            nc.vector.tensor_copy(out=tab_scales_sb[live, :].bitcast(I32), in_=tab_rows[live, :])
+        w2_scales_raw = held.tile([P, H], U8, name="w2_scales_raw", align_bytes=64)
+        nc.gpsimd.memset(w2_scales_raw[:].bitcast(I32), 0)
         w2_raw = held.tile([P, 2 * H], U8, name="w2_raw")
         nc.sync.dma_start(out=w2_raw[:].bitcast(I32), in_=w2_words[0].bitcast(I32))
-        w1_raw = load_weight(w1, 0, "w1_raw0", 4 * T)
+        w1_raw = load_weight(w1, 0, "w1_raw0", FIRST_WEIGHT_AT)
         tab_sb = staged.tile([P, T], I32, name="tab_sb", offset=0, align_bytes=64)
         nc.sync.dma_start(out=tab_sb[:], in_=tab_words[0].rearrange("p t i -> p (t i)").bitcast(I32))
+        nc.sync.dma_start(pos1_sb[:], pos1)
+        nc.sync.dma_start(pos2_sb[:], pos2)
+        for i in range(SCALE_ROWS):
+            nc.sync.dma_start(
+                out=w2_scales_raw[i:P:QUADRANT, :].bitcast(I32), in_=w2_scales[0, i:16:SCALE_ROWS, :].bitcast(I32)
+            )
         vec_rows = held.tile([P, PASSES, P], F32, name="vec_rows")
-        nc.vector.memset(vec_rows[:], 0.0)
+        nc.gpsimd.memset(vec_rows[:], 0.0)
         for n, vec in enumerate((gain, shift, wt)):
             nc.gpsimd.dma_start(out=vec_rows[n:P:QUADRANT], in_=vec.rearrange("(b q x) -> q b x", b=PASSES, x=P))
 
@@ -102,48 +119,50 @@ def tile_list_sense_link_scores_kernel(
             out=w2_codes[:].bitcast(I32).rearrange("p (b t g w) -> p b t g w", b=PASSES, t=PACK, w=2),
             in_=w2_raw[:].bitcast(I32).rearrange("p (b g t w) -> p b t g w", b=PASSES, t=PACK, w=2),
         )
-        v_plane = held.tile([P, S], U8, name="v_plane", align_bytes=64)
-        nc.vector.tensor_copy(v_plane[:], tab_plane[:].indirect(offs_sb[:]))
-        w2_scales_sb = held.tile([P, H], U8, name="w2_scales_sb", align_bytes=64)
-        nc.vector.tensor_copy(
-            out=w2_scales_sb[:].bitcast(I32).rearrange("p (b t g) -> p b t g", b=PASSES, t=PACK),
-            in_=w2_plane[:].bitcast(I32).rearrange("p (b g t) -> p b t g", b=PASSES, t=PACK),
-        )
+        v_scales = held.tile([P, S], U8, name="v_scales", align_bytes=64)
+        nc.vector.tensor_copy(v_scales[:], tab_scales_sb[:].indirect(offs_sb[:]))
         w1_q, w3_q = {}, {}
         w1_q[0] = (
-            early.tile([P, PASS], U32, name="w1_0_codes", offset=2 * PACK * PASS + H, align_bytes=64),
+            early.tile([P, PASS], U32, name="w1_0_codes", offset=TAB_SCALES_AT, align_bytes=64),
             held.tile([P, PASS], U8, name="w1_0_scales", align_bytes=64),
         )
-        quantise(w1_q[0], weave_weight(nc.scalar.copy, w1_raw, early.tile([P, PACK * PASS], BF16, name="w1_0", offset=0, align_bytes=64)), 0, PASS)
-        v_words = early.tile([P, S], U32, name="v_words", offset=H, align_bytes=64)
+        w1_grouped = early.tile([P, PACK * PASS], BF16, name="w1_0", offset=0, align_bytes=64)
+        weave_weight(w1_raw, w1_grouped)
+        quantise(w1_q[0], w1_grouped, 0, PASS)
+        v_words = early.tile([P, S], U32, name="v_words", offset=0, align_bytes=64)
         for half in range(HALVES):
             nc.vector.tensor_copy(
                 v_words[:, half * BANK : (half + 1) * BANK],
                 tab_sb[:].bitcast(U32).indirect(offs_sb[:, half * BANK // PER_COLUMN : (half + 1) * BANK // PER_COLUMN]),
             )
 
-        vec_dealt = held.tile([P, SLICES * QUADRANT], F32, name="vec_dealt", align_bytes=64)
-        nc.gpsimd.tensor_copy(
+        w2_scales_sb = staged.tile([P, H], U8, name="w2_scales_sb", offset=W2_SCALES_AT, align_bytes=64)
+        nc.vector.tensor_copy(
+            out=w2_scales_sb[:].bitcast(I32).rearrange("p (b t g) -> p b t g", b=PASSES, t=PACK),
+            in_=w2_scales_raw[:].bitcast(I32).rearrange("p (b g t) -> p b t g", b=PASSES, t=PACK),
+        )
+        vec_dealt = staged.tile([P, SLICES * QUADRANT], F32, name="vec_dealt", offset=VECTORS_AT, align_bytes=64)
+        nc.vector.tensor_copy(
             out=vec_dealt[:].rearrange("p (b t g e) -> p b t g e", b=PASSES, t=PACK, e=RUN),
             in_=vec_rows[:].rearrange("p b (g t e) -> p b t g e", t=PACK, e=RUN),
         )
-        channels = early.tile([P, SLICES * QUADRANT], F32, name="channels", offset=0, align_bytes=64)
+        channels = held.tile([P, SLICES * QUADRANT], F32, name="channels", align_bytes=64)
         nc.vector.transpose(channels[:], vec_dealt[:])
-        by_slice = channels[:].rearrange("p (s n) -> p n s", n=QUADRANT)
+        by_vector = channels[:].rearrange("p (s n) -> p n s", n=QUADRANT)
         times_wt = held.tile([P, 2, SLICES], F32, name="times_wt")
         for n in range(2):
-            nc.gpsimd.tensor_tensor(times_wt[:, n], by_slice[:, n], by_slice[:, 2], ALU.mult)
+            nc.gpsimd.tensor_tensor(times_wt[:, n], by_vector[:, n], by_vector[:, 2], ALU.mult)
 
-        def first_stage(codes, plane, half, tag):
-            acc = psum.tile([P, BANK], F32, name=tag, bufs=4 if tag == "bank_scalar" else 4)
+        def first_stage(codes, scales, half, tag):
+            acc = psum.tile([P, BANK], F32, name=tag)
             cols = slice(half * BANK, (half + 1) * BANK)
             nc.tensor.matmul_mx(
-                out=acc[:], lhsT=codes, lhsT_scale=plane,
-                rhs=v_words[:, cols].bitcast(FP8X4), rhs_scale=v_plane[:, cols], start=True, stop=True,
+                out=acc[:], lhsT=codes, lhsT_scale=scales,
+                rhs=v_words[:, cols].bitcast(FP8X4), rhs_scale=v_scales[:, cols], start=True, stop=True,
             )
             return acc
 
-        def columns(quantised, s):
+        def slice_columns(quantised, s):
             b, t = divmod(s, PACK)
             return quantised[b][0][:, t * P : (t + 1) * P].bitcast(FP8X4), quantised[b][1][:, t * P : (t + 1) * P]
 
@@ -151,20 +170,20 @@ def tile_list_sense_link_scores_kernel(
             return slots.tile([P, BANK], F32, name="%s%d_%d" % (name, s, half), offset=((s % DEPTH) * HALVES + half) * 4 * BANK)
 
         views, bents, sums, picked = {}, {}, {}, {}
-        x1_planes = [held.tile([P, PACK, L], BF16, name="x1_planes%d" % b) for b in range(PASSES)]
-        x2_planes = [held.tile([P, PACK, L], BF16, name="x2_planes%d" % b) for b in range(PASSES)]
-        x3_planes = {}
+        x1_rows = [held.tile([P, PACK, L], BF16, name="x1_rows%d" % b) for b in range(PASSES)]
+        x2_rows = [held.tile([P, PACK, L], BF16, name="x2_rows%d" % b) for b in range(PASSES)]
+        x3_rows = {}
         x1_q, x2_q, x3_q = {}, {}, {}
 
         def make_view(s):
-            views[s] = ring.tile([P, S], F32, name="view", bufs=5)
+            views[s] = ring.tile([P, S], F32, name="view", bufs=VIEW_BUFS)
             for half in range(HALVES):
-                acc = first_stage(*columns(w3_q, s), half, "bank_scalar")
+                acc = first_stage(*slice_columns(w3_q, s), half, "bank_scalar")
                 nc.scalar.copy(out=views[s][:, half * BANK : (half + 1) * BANK], in_=acc[:])
 
         def make_bent(s, halves=range(HALVES)):
             for half in halves:
-                acc = first_stage(*columns(w1_q, s), half, "bank_scalar")
+                acc = first_stage(*slice_columns(w1_q, s), half, "bank_scalar")
                 bents[s, half] = slot(s, half, "bent")
                 nc.scalar.activation(out=bents[s, half][:], in_=acc[:], func=ACT.Tanh)
 
@@ -177,43 +196,49 @@ def tile_list_sense_link_scores_kernel(
                 )
                 nc.vector.tensor_tensor(sums[s][:, half * BANK : (half + 1) * BANK], straight[:], bents[s, half][:], ALU.add)
 
-        def pick(s):
+        def pick_sum(s):
             for n, pos_sb in enumerate((pos1_sb, pos2_sb)):
                 picked[s, n] = slot(s + 1, n, "picked")
                 nc.vector.tensor_copy(picked[s, n][:], sums[s][:].indirect(pos_sb[:]))
 
         def pick_view(s):
             b, t = divmod(s, PACK)
-            nc.vector.tensor_copy(x3_planes[b][:, t, :], views[s][:].indirect(pos2_sb[:]))
+            nc.vector.tensor_copy(x3_rows[b][:, t, :], views[s][:].indirect(pos2_sb[:]))
+
+        def round_x1(s):
+            b, t = divmod(s, PACK)
+            nc.scalar.activation(
+                out=x1_rows[b][:, t, :], in_=picked[s, 0][:], func=ACT.Copy, scale=channels[:, QUADRANT * s : QUADRANT * s + 1]
+            )
 
         def round_x2(s):
             b, t = divmod(s, PACK)
             nc.scalar.activation(
-                out=x2_planes[b][:, t, :], in_=picked[s, 1][:], func=ACT.Identity,
+                out=x2_rows[b][:, t, :], in_=picked[s, 1][:], func=ACT.Identity,
                 scale=times_wt[:, 0, s : s + 1], bias=times_wt[:, 1, s : s + 1],
             )
 
-        def round_x1(s):
-            b, t = divmod(s, PACK)
-            nc.scalar.activation(out=x1_planes[b][:, t, :], in_=picked[s, 0][:], func=ACT.Copy, scale=channels[:, QUADRANT * s : QUADRANT * s + 1])
+        def round_both(s):
+            round_x1(s)
+            round_x2(s)
 
-        def later_weight(copy, raw, store, b, name):
+        def later_weight(w, b, store, name, offset):
+            raw = load_weight(w, b, name + "_raw", offset)
             store[b] = operand(name)
-            quantise(store[b], weave_weight(copy, raw, held.tile([P, PACK * PASS], BF16, name=name, align_bytes=64)), 0, PASS)
+            grouped = held.tile([P, PACK * PASS], BF16, name=name, align_bytes=64)
+            weave_weight(raw, grouped)
+            quantise(store[b], grouped, 0, PASS)
 
-        def rows_operand(copy, planes, store, b, name, parts=1):
+        def rows_operand(copy, by_slice_rows, name, parts):
             grouped = held.tile([P, L * PACK], BF16, name=name, align_bytes=64)
-            store[b] = operand(name)
+            target = operand(name)
             for part in range(parts):
-                weave_rows(copy, planes, grouped, part * L // parts, (part + 1) * L // parts)
+                weave_rows(copy, by_slice_rows, grouped, part * L // parts, (part + 1) * L // parts)
             for part in range(parts):
-                quantise(store[b], grouped, part * L // parts, (part + 1) * L // parts)
+                quantise(target, grouped, part * L // parts, (part + 1) * L // parts)
+            return target
 
-        def rows_part(copy, planes, target, grouped, c0, c1):
-            weave_rows(copy, planes, grouped, c0, c1)
-            quantise(target, grouped, c0, c1)
-
-        x3_planes[0] = held.tile([P, PACK, L], F32, name="x3_planes0")
+        x3_rows[0] = held.tile([P, PACK, L], F32, name="x3_rows0")
         make_bent(0, [0])
         make_bent(1, [0])
         make_sum(0, [0])
@@ -223,75 +248,77 @@ def tile_list_sense_link_scores_kernel(
         make_sum(0, [1])
         make_sum(1, [1])
         make_bent(2)
-        pick(0)
+
+        pick_sum(0)
         make_bent(3)
         make_sum(2)
-        later_weight(nc.scalar.copy, load_weight(w1, 1, "w1_raw1", 0), w1_q, 1, "w1_1")
-        pick(1)
-        round_x1(0)
-        round_x2(0)
-        later_weight(nc.scalar.copy, load_weight(w3, 0, "w3_raw0", 8192), w3_q, 0, "w3_0")
+        later_weight(w1, 1, w1_q, "w1_1", WEIGHT_A_AT)
+
+        pick_sum(1)
+        round_both(0)
+        later_weight(w3, 0, w3_q, "w3_0", WEIGHT_B_AT)
         make_sum(3)
-        pick(2)
-        round_x1(1)
-        round_x2(1)
+
+        pick_sum(2)
+        round_both(1)
         make_bent(4)
         make_bent(5)
         make_sum(4)
-        pick(3)
+
+        pick_sum(3)
         make_view(0)
-        later_weight(nc.scalar.copy, load_weight(w3, 1, "w3_raw1", 0), w3_q, 1, "w3_1")
-        round_x1(2)
-        round_x2(2)
+        later_weight(w3, 1, w3_q, "w3_1", WEIGHT_A_AT)
+        round_both(2)
         make_bent(6)
         make_sum(5)
-        pick(4)
+
+        pick_sum(4)
         make_view(1)
         pick_view(0)
         pick_view(1)
-        round_x1(3)
-        round_x2(3)
+        round_both(3)
         make_bent(7)
         make_sum(6)
-        rows_operand(nc.vector.tensor_copy, x2_planes[0], x2_q, 0, "x2_0", 2)
-        pick(5)
+        x2_q[0] = rows_operand(nc.vector.tensor_copy, x2_rows[0], "x2_0", 2)
+
+        pick_sum(5)
         make_view(2)
         make_view(3)
         pick_view(2)
         pick_view(3)
-        round_x1(4)
-        round_x2(4)
+        round_both(4)
         make_sum(7)
-        pick(6)
-        pick(7)
-        rel_sb = staged.tile([P, L], F32, name="rel_sb", offset=0, align_bytes=64)
+
+        pick_sum(6)
+        pick_sum(7)
+
+        rel_sb = staged.tile([P, L], F32, name="rel_sb", offset=WEIGHT_A_AT, align_bytes=64)
         nc.sync.dma_start(out=rel_sb[:], in_=rel.partition_broadcast(P))
         make_view(4)
         make_view(5)
-        round_x1(5)
-        round_x2(5)
+        round_both(5)
         make_view(6)
-        rows_operand(nc.scalar.copy, x1_planes[0], x1_q, 0, "x1_0")
-        rows_operand(nc.scalar.copy, x3_planes[0], x3_q, 0, "x3_0")
+        x1_q[0] = rows_operand(nc.scalar.copy, x1_rows[0], "x1_0", 1)
+        x3_q[0] = rows_operand(nc.scalar.copy, x3_rows[0], "x3_0", 1)
         make_view(7)
-        round_x1(6)
-        round_x2(6)
-        round_x1(7)
+        round_both(6)
+
+        round_x1(SLICES - 1)
         x1_q[1] = operand("x1_1")
-        x1_last = held.tile([P, L * PACK], BF16, name="x1_1", align_bytes=64)
-        rows_part(nc.scalar.copy, x1_planes[1], x1_q[1], x1_last, 0, L // 2)
-        round_x2(7)
-        rows_operand(nc.scalar.copy, x2_planes[1], x2_q, 1, "x2_1")
-        rows_part(nc.scalar.copy, x1_planes[1], x1_q[1], x1_last, L // 2, L)
-        x3_planes[1] = totals.tile([P, PACK, L], F32, name="x3_planes1", offset=0)
-        pick_view(4)
-        pick_view(5)
-        pick_view(6)
-        pick_view(7)
-        rows_operand(nc.vector.tensor_copy, x3_planes[1], x3_q, 1, "x3_1", 2)
+        x1_grouped = held.tile([P, L * PACK], BF16, name="x1_1", align_bytes=64)
+        weave_rows(nc.scalar.copy, x1_rows[1], x1_grouped, 0, L // 2)
+        quantise(x1_q[1], x1_grouped, 0, L // 2)
+        round_x2(SLICES - 1)
+        x2_q[1] = rows_operand(nc.scalar.copy, x2_rows[1], "x2_1", 1)
+        weave_rows(nc.scalar.copy, x1_rows[1], x1_grouped, L // 2, L)
+        quantise(x1_q[1], x1_grouped, L // 2, L)
+        x3_rows[1] = totals.tile([P, PACK, L], F32, name="x3_rows1", offset=0)
+        for s in range(PACK, SLICES):
+            pick_view(s)
+        x3_q[1] = rows_operand(nc.vector.tensor_copy, x3_rows[1], "x3_1", 2)
 
         def second_stage(rhs_q, mc, tag):
-            acc = psum.tile([P, BANK], F32, name=tag, bufs=4 if tag == "bank_scalar" else 4)
+            acc = psum.tile([P, BANK], F32, name=tag)
             cols = slice(mc * P, (mc + 1) * P)
             for b in range(PASSES):
                 nc.tensor.matmul_mx(
@@ -300,13 +327,14 @@ def tile_list_sense_link_scores_kernel(
                 )
             return acc
 
-        e_sb = {}
-        for mc in range(L // P):
-            e_sb[mc] = ring.tile([P, L], F32, name="e_sb")
-            nc.scalar.copy(out=e_sb[mc][:], in_=second_stage(x3_q, mc, "bank_scalar")[:])
-        for mc in range(L // P):
-            larger = ring.tile([P, L], F32, name="larger")
-            nc.vector.tensor_tensor(larger[:], second_stage(x2_q, mc, "bank_vector")[:], e_sb[mc][:], ALU.max)
-            scored = ring.tile([P, L], F32, name="scored")
-            (nc.gpsimd if mc < 0 else nc.vector).tensor_tensor(scored[:], larger[:], rel_sb[:], ALU.mult)
+        e3_sb = [tail.tile([P, L], F32, name="e3_sb%d" % mc, offset=mc * 4 * L) for mc in range(CHUNKS)]
+        larger = [ring.tile([P, L], F32, name="larger") for mc in range(CHUNKS)]
+        for mc in range(CHUNKS):
+            nc.scalar.copy(out=e3_sb[mc][:], in_=second_stage(x3_q, mc, "bank_scalar")[:])
+        for mc in range(CHUNKS):
+            nc.vector.tensor_tensor(larger[mc][:], second_stage(x2_q, mc, "bank_vector")[:], e3_sb[mc][:], ALU.max)
+        for mc in range(CHUNKS):
+            place = mc + 1 if mc == 1 else mc + CHUNKS
+            scored = tail.tile([P, L], F32, name="scored%d" % mc, offset=place * 4 * L)
+            (nc.gpsimd if mc == 0 else nc.vector).tensor_tensor(scored[:], larger[mc][:], rel_sb[:], ALU.mult)
             nc.sync.dma_start(out=out[mc * P : (mc + 1) * P, :], in_=scored[:])

from contextlib import ExitStack

import concourse.mybir as mybir

K, H, T, S, L = 512, 1024, 4096, 1024, 512
FLOPS = 3 * 2 * K * H * S + 2 * 2 * H * L * L

F32 = mybir.dt.float32
BF16 = mybir.dt.bfloat16
I32 = mybir.dt.int32
U32 = mybir.dt.uint32
U16 = mybir.dt.uint16
U8 = mybir.dt.uint8
FP8X4 = mybir.dt.float8_e4m3fn_x4
FP4X4 = mybir.dt.float4_e2m1fn_x4
ACT = mybir.ActivationFunctionType
ALU = mybir.AluOpType

P = 128
PACK = 4
PASS = P * PACK
PASSES = H // PASS
SLICES = PASSES * PACK
BANK = 512
HALVES = S // BANK
RUN = 4
PER_COLUMN = 16
QUADRANT = 32
SCALE_ROWS = 4
DEPTH = 3
VIEW_BUFS = 5
CHUNKS = L // P

FIRST_WEIGHT_AT = 4 * T
W2_SCALES_AT = 0
VECTORS_AT = H
WEIGHT_A_AT = 2 * H
WEIGHT_B_AT = WEIGHT_A_AT + 4 * PACK * PASS
TAB_SCALES_AT = 2 * PACK * PASS


def tile_list_sense_link_scores_kernel(
    tc, tab_words, tab_scales, offs, pos1, pos2, w1, w2_words, w2_scales, w3, gain, shift, wt, rel, out
):
    nc = tc.nc
    with ExitStack() as ctx:
        lists = ctx.enter_context(tc.tile_pool(name="lists", bufs=1))
        held = ctx.enter_context(tc.tile_pool(name="held", bufs=1))
        staged = ctx.enter_context(tc.tile_pool(name="staged", bufs=1))
        tail = ctx.enter_context(tc.tile_pool(name="tail", bufs=1))
        early = ctx.enter_context(tc.tile_pool(name="early", bufs=1))
        totals = ctx.enter_context(tc.tile_pool(name="totals", bufs=1))
        slots = ctx.enter_context(tc.tile_pool(name="slots", bufs=1))
        ring = ctx.enter_context(tc.tile_pool(name="ring", bufs=CHUNKS))
        psum = ctx.enter_context(tc.psum_pool(name="psum", bufs=4))

        def load_weight(w, b, name, offset):
            raw = staged.tile([P, PACK, PASS], F32, name=name, offset=offset, align_bytes=64)
            nc.sync.dma_start(out=raw[:], in_=w.rearrange("(p j) c -> p j c", j=PACK)[:, :, b * PASS : (b + 1) * PASS])
            return raw

        def weave_weight(raw, grouped):
            nc.scalar.copy(
                out=grouped[:].rearrange("p (t g e j) -> p g t j e", t=PACK, e=RUN, j=PACK),
                in_=raw[:].rearrange("p j (g t e) -> p g t j e", t=PACK, e=RUN),
            )

        def weave_rows(copy, by_slice_rows, grouped, c0, c1):
            copy(
                out=grouped[:, c0 * PACK : c1 * PACK].rearrange("p (c i t) -> p c t i", i=RUN, t=PACK),
                in_=by_slice_rows[:, :, c0:c1].rearrange("p t (c i) -> p c t i", i=RUN),
            )

        def operand(name):
            codes = held.tile([P, L], U32, name=name + "_codes", align_bytes=64)
            scales = held.tile([P, L], U8, name=name + "_scales", align_bytes=64)
            return codes, scales

        def quantise(target, grouped, c0, c1):
            nc.vector.quantize_mx(
                out=target[0][:, c0:c1].bitcast(FP8X4), scales=target[1][:, c0:c1], in_=grouped[:, c0 * PACK : c1 * PACK]
            )

        offs_sb = lists.tile([P, S // PER_COLUMN], U16, name="offs_sb")
        pos1_sb = lists.tile([P, L // PER_COLUMN], U16, name="pos1_sb")
        pos2_sb = lists.tile([P, L // PER_COLUMN], U16, name="pos2_sb")
        nc.sync.dma_start(offs_sb[:], offs)
        tab_rows = held.tile([P, T // 4], I32, name="tab_rows")
        for q in range(P // QUADRANT):
            nc.sync.dma_start(
                out=tab_rows[QUADRANT * q : QUADRANT * q + SCALE_ROWS, :],
                in_=tab_scales[0, SCALE_ROWS * q : SCALE_ROWS * (q + 1), :].bitcast(I32),
            )
        tab_scales_sb = early.tile([P, T], U8, name="tab_scales_sb", offset=TAB_SCALES_AT, align_bytes=64)
        nc.vector.memset(tab_scales_sb[:].bitcast(I32), 0)
        for q in range(P // QUADRANT):
            live = slice(QUADRANT * q, QUADRANT * q + SCALE_ROWS)
            nc.vector.tensor_copy(out=tab_scales_sb[live, :].bitcast(I32), in_=tab_rows[live, :])
        w2_scales_raw = held.tile([P, H], U8, name="w2_scales_raw", align_bytes=64)
        nc.gpsimd.memset(w2_scales_raw[:].bitcast(I32), 0)
        w2_raw = held.tile([P, 2 * H], U8, name="w2_raw")
        nc.sync.dma_start(out=w2_raw[:].bitcast(I32), in_=w2_words[0].bitcast(I32))
        w1_raw = load_weight(w1, 0, "w1_raw0", FIRST_WEIGHT_AT)
        tab_sb = staged.tile([P, T], I32, name="tab_sb", offset=0, align_bytes=64)
        nc.sync.dma_start(out=tab_sb[:], in_=tab_words[0].rearrange("p t i -> p (t i)").bitcast(I32))
        nc.sync.dma_start(pos1_sb[:], pos1)
        nc.sync.dma_start(pos2_sb[:], pos2)
        for i in range(SCALE_ROWS):
            nc.sync.dma_start(
                out=w2_scales_raw[i:P:QUADRANT, :].bitcast(I32), in_=w2_scales[0, i:16:SCALE_ROWS, :].bitcast(I32)
            )
        vec_rows = held.tile([P, PASSES, P], F32, name="vec_rows")
        nc.gpsimd.memset(vec_rows[:], 0.0)
        for n, vec in enumerate((gain, shift, wt)):
            nc.gpsimd.dma_start(out=vec_rows[n:P:QUADRANT], in_=vec.rearrange("(b q x) -> q b x", b=PASSES, x=P))

        w2_codes = held.tile([P, 2 * H], U8, name="w2_codes", align_bytes=64)
        nc.vector.tensor_copy(
            out=w2_codes[:].bitcast(I32).rearrange("p (b t g w) -> p b t g w", b=PASSES, t=PACK, w=2),
            in_=w2_raw[:].bitcast(I32).rearrange("p (b g t w) -> p b t g w", b=PASSES, t=PACK, w=2),
        )
        v_scales = held.tile([P, S], U8, name="v_scales", align_bytes=64)
        nc.vector.tensor_copy(v_scales[:], tab_scales_sb[:].indirect(offs_sb[:]))
        w1_q, w3_q = {}, {}
        w1_q[0] = (
            early.tile([P, PASS], U32, name="w1_0_codes", offset=TAB_SCALES_AT, align_bytes=64),
            held.tile([P, PASS], U8, name="w1_0_scales", align_bytes=64),
        )
        w1_grouped = early.tile([P, PACK * PASS], BF16, name="w1_0", offset=0, align_bytes=64)
        weave_weight(w1_raw, w1_grouped)
        quantise(w1_q[0], w1_grouped, 0, PASS)
        v_words = early.tile([P, S], U32, name="v_words", offset=0, align_bytes=64)
        for half in range(HALVES):
            nc.vector.tensor_copy(
                v_words[:, half * BANK : (half + 1) * BANK],
                tab_sb[:].bitcast(U32).indirect(offs_sb[:, half * BANK // PER_COLUMN : (half + 1) * BANK // PER_COLUMN]),
            )

        w2_scales_sb = staged.tile([P, H], U8, name="w2_scales_sb", offset=W2_SCALES_AT, align_bytes=64)
        nc.vector.tensor_copy(
            out=w2_scales_sb[:].bitcast(I32).rearrange("p (b t g) -> p b t g", b=PASSES, t=PACK),
            in_=w2_scales_raw[:].bitcast(I32).rearrange("p (b g t) -> p b t g", b=PASSES, t=PACK),
        )
        vec_dealt = staged.tile([P, SLICES * QUADRANT], F32, name="vec_dealt", offset=VECTORS_AT, align_bytes=64)
        nc.vector.tensor_copy(
            out=vec_dealt[:].rearrange("p (b t g e) -> p b t g e", b=PASSES, t=PACK, e=RUN),
            in_=vec_rows[:].rearrange("p b (g t e) -> p b t g e", t=PACK, e=RUN),
        )
        channels = held.tile([P, SLICES * QUADRANT], F32, name="channels", align_bytes=64)
        nc.vector.transpose(channels[:], vec_dealt[:])
        by_vector = channels[:].rearrange("p (s n) -> p n s", n=QUADRANT)
        times_wt = held.tile([P, 2, SLICES], F32, name="times_wt")
        for n in range(2):
            nc.gpsimd.tensor_tensor(times_wt[:, n], by_vector[:, n], by_vector[:, 2], ALU.mult)

        def first_stage(codes, scales, half, tag):
            acc = psum.tile([P, BANK], F32, name=tag)
            cols = slice(half * BANK, (half + 1) * BANK)
            nc.tensor.matmul_mx(
                out=acc[:], lhsT=codes, lhsT_scale=scales,
                rhs=v_words[:, cols].bitcast(FP8X4), rhs_scale=v_scales[:, cols], start=True, stop=True,
            )
            return acc

        def slice_columns(quantised, s):
            b, t = divmod(s, PACK)
            return quantised[b][0][:, t * P : (t + 1) * P].bitcast(FP8X4), quantised[b][1][:, t * P : (t + 1) * P]

        def slot(s, half, name):
            return slots.tile([P, BANK], F32, name="%s%d_%d" % (name, s, half), offset=((s % DEPTH) * HALVES + half) * 4 * BANK)

        views, bents, sums, picked = {}, {}, {}, {}
        x1_rows = [held.tile([P, PACK, L], BF16, name="x1_rows%d" % b) for b in range(PASSES)]
        x2_rows = [held.tile([P, PACK, L], BF16, name="x2_rows%d" % b) for b in range(PASSES)]
        x3_rows = {}
        x1_q, x2_q, x3_q = {}, {}, {}

        def make_view(s):
            views[s] = ring.tile([P, S], F32, name="view", bufs=VIEW_BUFS)
            for half in range(HALVES):
                acc = first_stage(*slice_columns(w3_q, s), half, "bank_scalar")
                nc.scalar.copy(out=views[s][:, half * BANK : (half + 1) * BANK], in_=acc[:])

        def make_bent(s, halves=range(HALVES)):
            for half in halves:
                acc = first_stage(*slice_columns(w1_q, s), half, "bank_scalar")
                bents[s, half] = slot(s, half, "bent")
                nc.scalar.activation(out=bents[s, half][:], in_=acc[:], func=ACT.Tanh)

        def make_sum(s, halves=range(HALVES)):
            if s not in sums:
                sums[s] = totals.tile([P, S], F32, name="sum%d" % s, offset=(1 + s % DEPTH) * 4 * S)
            for half in halves:
                straight = first_stage(
                    w2_codes[:, 2 * s * P : 2 * (s + 1) * P].bitcast(FP4X4), w2_scales_sb[:, s * P : (s + 1) * P], half, "bank_vector"
                )
                nc.vector.tensor_tensor(sums[s][:, half * BANK : (half + 1) * BANK], straight[:], bents[s, half][:], ALU.add)

        def pick_sum(s):
            for n, pos_sb in enumerate((pos1_sb, pos2_sb)):
                picked[s, n] = slot(s + 1, n, "picked")
                nc.vector.tensor_copy(picked[s, n][:], sums[s][:].indirect(pos_sb[:]))

        def pick_view(s):
            b, t = divmod(s, PACK)
            nc.vector.tensor_copy(x3_rows[b][:, t, :], views[s][:].indirect(pos2_sb[:]))

        def round_x1(s):
            b, t = divmod(s, PACK)
            nc.scalar.activation(
                out=x1_rows[b][:, t, :], in_=picked[s, 0][:], func=ACT.Copy, scale=channels[:, QUADRANT * s : QUADRANT * s + 1]
            )

        def round_x2(s):
            b, t = divmod(s, PACK)
            nc.scalar.activation(
                out=x2_rows[b][:, t, :], in_=picked[s, 1][:], func=ACT.Identity,
                scale=times_wt[:, 0, s : s + 1], bias=times_wt[:, 1, s : s + 1],
            )

        def round_both(s):
            round_x1(s)
            round_x2(s)

        def later_weight(w, b, store, name, offset):
            raw = load_weight(w, b, name + "_raw", offset)
            store[b] = operand(name)
            grouped = held.tile([P, PACK * PASS], BF16, name=name, align_bytes=64)
            weave_weight(raw, grouped)
            quantise(store[b], grouped, 0, PASS)

        def rows_operand(copy, by_slice_rows, name, parts):
            grouped = held.tile([P, L * PACK], BF16, name=name, align_bytes=64)
            target = operand(name)
            for part in range(parts):
                weave_rows(copy, by_slice_rows, grouped, part * L // parts, (part + 1) * L // parts)
            for part in range(parts):
                quantise(target, grouped, part * L // parts, (part + 1) * L // parts)
            return target

        x3_rows[0] = held.tile([P, PACK, L], F32, name="x3_rows0")
        make_bent(0, [0])
        make_bent(1, [0])
        make_sum(0, [0])
        make_bent(0, [1])
        make_sum(1, [0])
        make_bent(1, [1])
        make_sum(0, [1])
        make_sum(1, [1])
        make_bent(2)

        pick_sum(0)
        make_bent(3)
        make_sum(2)
        later_weight(w1, 1, w1_q, "w1_1", WEIGHT_A_AT)

        pick_sum(1)
        round_both(0)
        later_weight(w3, 0, w3_q, "w3_0", WEIGHT_B_AT)
        make_sum(3)

        pick_sum(2)
        round_both(1)
        make_bent(4)
        make_bent(5)
        make_sum(4)

        pick_sum(3)
        make_view(0)
        later_weight(w3, 1, w3_q, "w3_1", WEIGHT_A_AT)
        round_both(2)
        make_bent(6)
        make_sum(5)

        pick_sum(4)
        make_view(1)
        pick_view(0)
        pick_view(1)
        round_both(3)
        make_bent(7)
        make_sum(6)
        x2_q[0] = rows_operand(nc.vector.tensor_copy, x2_rows[0], "x2_0", 2)

        pick_sum(5)
        make_view(2)
        make_view(3)
        pick_view(2)
        pick_view(3)
        round_both(4)
        make_sum(7)

        pick_sum(6)
        pick_sum(7)

        rel_sb = staged.tile([P, L], F32, name="rel_sb", offset=WEIGHT_A_AT, align_bytes=64)
        nc.sync.dma_start(out=rel_sb[:], in_=rel.partition_broadcast(P))
        make_view(4)
        make_view(5)
        round_both(5)
        make_view(6)
        x1_q[0] = rows_operand(nc.scalar.copy, x1_rows[0], "x1_0", 1)
        x3_q[0] = rows_operand(nc.scalar.copy, x3_rows[0], "x3_0", 1)
        make_view(7)
        round_both(6)

        round_x1(SLICES - 1)
        x1_q[1] = operand("x1_1")
        x1_grouped = held.tile([P, L * PACK], BF16, name="x1_1", align_bytes=64)
        weave_rows(nc.scalar.copy, x1_rows[1], x1_grouped, 0, L // 2)
        quantise(x1_q[1], x1_grouped, 0, L // 2)
        round_x2(SLICES - 1)
        x2_q[1] = rows_operand(nc.scalar.copy, x2_rows[1], "x2_1", 1)
        weave_rows(nc.scalar.copy, x1_rows[1], x1_grouped, L // 2, L)
        quantise(x1_q[1], x1_grouped, L // 2, L)
        x3_rows[1] = totals.tile([P, PACK, L], F32, name="x3_rows1", offset=0)
        for s in range(PACK, SLICES):
            pick_view(s)
        x3_q[1] = rows_operand(nc.vector.tensor_copy, x3_rows[1], "x3_1", 2)

        def second_stage(rhs_q, mc, tag):
            acc = psum.tile([P, BANK], F32, name=tag)
            cols = slice(mc * P, (mc + 1) * P)
            for b in range(PASSES):
                nc.tensor.matmul_mx(
                    out=acc[:], lhsT=x1_q[b][0][:, cols].bitcast(FP8X4), lhsT_scale=x1_q[b][1][:, cols],
                    rhs=rhs_q[b][0][:].bitcast(FP8X4), rhs_scale=rhs_q[b][1][:], start=(b == 0), stop=(b == PASSES - 1),
                )
            return acc

        e3_sb = [tail.tile([P, L], F32, name="e3_sb%d" % mc, offset=mc * 4 * L) for mc in range(CHUNKS)]
        larger = [ring.tile([P, L], F32, name="larger") for mc in range(CHUNKS)]
        for mc in range(CHUNKS):
            nc.scalar.copy(out=e3_sb[mc][:], in_=second_stage(x3_q, mc, "bank_scalar")[:])
        for mc in range(CHUNKS):
            nc.vector.tensor_tensor(larger[mc][:], second_stage(x2_q, mc, "bank_vector")[:], e3_sb[mc][:], ALU.max)
        for mc in range(CHUNKS):
            place = mc + 1 if mc == 1 else mc + CHUNKS
            scored = tail.tile([P, L], F32, name="scored%d" % mc, offset=place * 4 * L)
            (nc.gpsimd if mc == 0 else nc.vector).tensor_tensor(scored[:], larger[mc][:], rel_sb[:], ALU.mult)
            nc.sync.dma_start(out=out[mc * P : (mc + 1) * P, :], in_=scored[:])
